import numpy as np, ml_dtypes
CORES = [48,51,52,55]
N = 4
BF = ml_dtypes.bfloat16
V, S, Q, RO, W = 2048, 8, 256, 6, 3328
def pack(res, cap, B, T, K, wt, ka):
    w = B + 4096 * T - 65536 * K
    return {"res": np.ascontiguousarray(res).reshape(N, 128, W).astype(np.float32).astype(BF), "cap": np.ascontiguousarray(cap).reshape(N, 128, V).astype(np.float32).astype(BF),
            "br": np.ascontiguousarray(w).reshape(N, 128, V).astype(np.int32), "wt": np.ascontiguousarray(wt).reshape(N, 128, 1).astype(np.int32), "ka": np.ascontiguousarray(ka).reshape(N, 128, 1).astype(np.int32)}
def parts(rng):
    sh = (N, 8, 16, V)
    res = (rng.integers(4, 29, (N, 8, 1, W)) * rng.random((N, 8, 16, W))).astype(np.int64)
    heavy = (rng.random((N, 8, 1, W)) < 0.06) & (rng.random((N, 8, 16, W)) < 0.7)
    res = np.where(heavy, rng.integers(0, 256, res.shape), res)
    cap = rng.integers(0, 64, sh); dead = rng.choice(np.array([0.0, 0.25, 0.5]), (N, 8, 1, 1))
    B = rng.integers(0, W, sh); T = np.where(rng.random(sh) < dead, 0, rng.integers(0, 16, sh)); K = np.where(rng.random(sh) < 0.5, 0, rng.integers(0, 16, sh))
    return res, cap, B, T, K, rng.integers(0, 256, (N, 8, 16, 1)), rng.integers(0, V, (N, 8, 16, 1))
def setup_inputs(rng):
    return pack(*parts(rng))
def setup_inputs_corners(rng):
    res, cap, B, T, K, wt, ka = parts(rng)
    v = np.arange(V); t0 = v % S + 1; row = np.arange(16).reshape(16, 1)
    res[..., W - 16:] = np.where(row < np.arange(16), 200, 0)
    res[:, 5, :, 0:V:2] = 255; res[:, 6, :, 0:V:2] = 0; cap[:, 6, :, ::2] = 63
    cl = rng.integers(0, 9, (N, 8, 1, V)); one = rng.integers(0, 16, (N, 8, 1, V)); near = W - 16 + rng.integers(3, 7, (N, 8, 1, V)); same = rng.integers(0, W, (N, 8, 1, V))
    T = np.where(cl == 0, t0 - 1, T); K = np.where(cl == 0, 0, K)
    T = np.where(cl == 1, 15, T); K = np.where(cl == 1, 0, K)
    T = np.where(cl == 2, np.where(row % 2 == 0, t0, t0 - 1), T); K = np.where(cl == 2, 0, K)
    T = np.where(cl == 3, 15, T); K = np.where(cl == 3, np.where(row % 2 == 0, t0 - 1, t0), K)
    T = np.where(cl == 4, np.where(row == one, 15, 0), T); K = np.where(cl == 4, 0, K); B = np.where(cl == 4, near, B); cap = np.where(cl == 4, 63, cap)
    T = np.where(cl == 5, 15, T); K = np.where(cl == 5, 0, K); B = np.where(cl == 5, same, B)
    cap = np.where(cl == 5, np.minimum(np.take_along_axis(res, same, 3), 63), cap)
    chain = np.where(row == 0, v, np.where(row == 1, np.maximum(v - 1, 0), np.where(row == 2, W - 1, np.where(row == 3, 0, V))))
    T = np.where(cl == 6, np.where(row < 5, 15, 0), T); K = np.where(cl == 6, 0, K); B = np.where(cl == 6, chain, B)
    two = (cl == 7) & ((row == 3) | (row == 15))
    T = np.where(two, 15, T); K = np.where(two, 0, K); B = np.where(two, near, B); cap = np.where(cl == 7, 63, cap)
    q = rng.permutation(N); T[q[0], 7] = 0; T[q[1], 7] = 15; K[q[1], 7] = 0
    wt[:, 0] = 0; wt[:, 1] = 255; ka[:, 2] = 0; ka[:, 3] = V - 1; ka[:, 4] = rng.choice(np.array([0, V >> 1]), (N, 16, 1))
    return pack(res, cap, B, T, K, wt, ka)
def setup_inputs_ends(rng):
    sh = (N, 8, 16, V); lane = np.arange(16).reshape(16, 1)
    kd = rng.choice(6, (N, 8, 1, W), p=[0.38, 0.12, 0.25, 0.1, 0.08, 0.07])
    kd[:, :, 0, W - 1] = np.where(np.arange(8) % 2 == 1, 1, 2); kd[:, 7, 0, V - 1] = 5; kd[:, 7, 0, V - 2] = 4
    rot = (lane + rng.integers(0, 16, (N, 8, 1, W))) % 16; some = 255 * (rng.random((N, 8, 16, W)) < 0.2)
    res = np.where(kd == 1, 255, np.where(kd == 2, some, np.where(kd == 3, 63, np.where(kd == 4, np.where(rot < 4, 255, 63), np.where(kd == 5, np.where(rot < 5, 255, 63), 0)))))
    ck = rng.choice(3, (N, 8, 1, V), p=[0.5, 0.15, 0.35]); cap = np.where(ck == 0, 63, np.where(ck == 1, 0, 63 * rng.integers(0, 2, sh)))
    up = rng.random(sh) < rng.choice(np.array([0.0, 0.1, 0.2]), (N, 8, 1, V))
    B = np.where(up, W - 1, 0); T = np.where(up, 15, 0); K = np.where(up, 0, 15)
    fr = rng.random(sh) < rng.choice(np.array([0.0, 0.1, 0.2, 0.4]), (N, 8, 1, V)); live = rng.random(sh) < 0.8
    B = np.where(fr, np.where(rng.random(sh) < 0.7, rng.integers(0, W, sh), rng.choice(np.array([0, V - 1, V, W - 1]), sh)), B)
    T = np.where(fr, np.where(live, 15, 15 * rng.integers(0, 2, sh)), T); K = np.where(fr, np.where(live, 0, 15 * rng.integers(0, 2, sh)), K)
    for j, first, col, c in ((0, 15, V - 1, 63), (1, 15, V - 2, 63), (2, 14, W - 1, 0)):
        a = S * (Q - 1 - j)
        B[:, 7, :, a:a + S] = 0; T[:, 7, :, a:a + S] = 0; K[:, 7, :, a:a + S] = 15; cap[:, 7, :, a:a + S] = c
        B[:, 7, first:, a:a + S] = col; T[:, 7, first:, a:a + S] = 15; K[:, 7, first:, a:a + S] = 0
    wt = np.where(rng.random((N, 8, 16, 1)) < 0.8, 255 * rng.integers(0, 2, (N, 8, 16, 1)), rng.integers(0, 256, (N, 8, 16, 1))); wt[:, 7] = 255; wt[:, 0, 0] = 0
    ka = np.where(rng.random((N, 8, 16, 1)) < 0.8, (V - 1) * rng.integers(0, 2, (N, 8, 16, 1)), rng.integers(0, V, (N, 8, 16, 1)))
    ka[:, 7] = rng.integers(0, V, (N, 16, 1)); ka[:, 0, 0] = 0; ka[:, 0, 1] = V - 1; ka[:, 7, 15] = V - 1
    return pack(res, cap, B, T, K, wt, ka)
def setup_inputs_full(rng):
    res, cap, B, T, K, wt, ka = parts(rng); q = rng.permutation(N); i = np.arange(Q); lane = np.arange(16).reshape(16, 1)
    res[..., W - 16:] = np.where(lane < np.arange(16), 200, 0)
    a = q[0]; T[a, :, :, 0::S] = 0; T[a, :, :, 1::S] = 0; cap[a, :, :, 1::S] = 63
    odd = rng.permutation(8 * Q)[:2 * int(rng.integers(1, 100)) + 1]; k = rng.integers(0, 16, odd.size); g = odd // Q; v = S * (odd % Q)
    B[a, g, k, v] = W - 16 + rng.integers(6, 16, odd.size); T[a, g, k, v] = 15; K[a, g, k, v] = 0
    a = q[1]; hit = lane == rng.integers(0, 16, (8, 1, Q))
    B[a, :, :, 0::S] = np.where(hit, W - 16 + rng.integers(6, 16, (8, 1, Q)), B[a, :, :, 0::S]); T[a, :, :, 0::S] = np.where(hit, 15, T[a, :, :, 0::S]); K[a, :, :, 0::S] = np.where(hit, 0, K[a, :, :, 0::S])
    for a, s in ((q[0], 2), (q[1], 1)):
        five = rng.random((8, 1, Q)) < 0.6; hit = lane == rng.integers(0, 16, (8, 1, Q))
        B[a, :, :, s::S] = np.where(five & hit, W - 11, B[a, :, :, s::S]); K[a, :, :, s::S] = np.where(five & hit, 0, K[a, :, :, s::S])
        T[a, :, :, s::S] = np.where(five, np.where(hit, 15, 0), T[a, :, :, s::S])
    a = q[2]; T[a] = 15; K[a] = 0; B[a, 1::2] = rng.integers(V, W, (4, 16, V))
    for g in (0, 4):
        base = rng.integers(200, 249, 16); turn = (lane + rng.integers(0, 16, (1, Q - 16))) % 16
        res[a, g, :, W - Q:W - 16] = base[turn] + (lane < rng.integers(0, 8, (1, Q - 16)))
        B[a, g] = np.where(rng.random((1, V)) < 0.5, rng.integers(W - Q, W - 16, (16, V)), B[a, g])
    a = q[3]; r = (a + 1) % N; T[a, :, :, 0::S] = 0
    for g in range(8):
        x, y = rng.permutation(16)[:2]; wt[r, g] = 0; wt[r, g, x] = 16; wt[r, g, y] = 1
        if g != 3: ka[r, g] = int(ka[r, g, 0, 0])
        o = rng.permutation(4096); p = ((o * o >> 5) + int(ka[r, g, 0, 0]) * o) & (V - 1)
        first = rng.permutation(np.unique(p, return_index=True)[1]); n = (Q, 8, Q, 1, Q, 8, Q, 1)[g]
        s = (o[first[rng.permutation(Q) % n]] - 37 * i) & 4095; col = V + rng.permutation(Q); k = rng.integers(0, 16, Q)
        res[a, g, :, V:V + Q] = 0; res[a, g, x, col] = s >> 4; res[a, g, y, col] = s & 15
        B[a, g, k, S * i] = col; T[a, g, k, S * i] = 15; K[a, g, k, S * i] = 0
    return pack(res, cap, B, T, K, wt, ka)
def setup_inputs_spread(rng):
    res, cap, B, T, K, wt, ka = parts(rng)
    res = (np.exp2(8 * rng.random((N, 8, 1, W)) ** 3) * rng.random((N, 8, 16, W))).astype(np.int64)
    res = np.where(rng.random((N, 8, 1, W)) < 0.02, rng.integers(0, 256, res.shape), np.minimum(res, 255))
    cap = np.minimum((np.exp2(6 - 6 * rng.random((N, 8, 1, V)) ** 3) * rng.random(cap.shape)).astype(np.int64), 63)
    B = np.minimum((W * rng.random(B.shape) ** rng.choice(np.array([0.5, 1.0, 3.0]), (N, 8, 1, 1))).astype(np.int64), W - 1)
    wt = np.minimum(np.exp2(8 * rng.random(wt.shape)).astype(np.int64), 255)
    return pack(res, cap, B, T, K, wt, ka)
def setup_inputs_ties(rng):
    res, cap, B, T, K, wt, ka = parts(rng)
    lane = np.arange(16).reshape(16, 1); turn = (lane + rng.integers(0, 16, (N, 8, 1, W))) % 16
    res = np.where(turn < rng.integers(2, 4, (N, 8, 1, W)), 40, 0)
    cap = np.broadcast_to(rng.choice(np.array([0, 20, 20, 39, 40, 63]), (N, 8, 1, V)), cap.shape)
    live = rng.random(B.shape) < rng.choice(np.array([0.1, 0.2, 0.3]), (N, 8, 1, 1))
    T = np.where(live, 15, 0); K = np.where(live, 0, K)
    wt[:, ::2] = 1; ka[:, 1::2] = rng.choice(np.array([0, 1, V >> 1, V - 1]), (N, 4, 16, 1))
    return pack(res, cap, B, T, K, wt, ka)
def check_inputs(d):
    bad = []
    for k, lo, hi in (("res", 0, 255), ("cap", 0, 63), ("br", -983040, 64767), ("wt", 0, 255), ("ka", 0, V - 1)):
        v = np.asarray(d[k]).astype(np.float64)
        if not np.all((v >= lo) & (v <= hi) & (v == np.floor(v))): bad.append("range of " + k)
    if np.any((np.asarray(d["br"]).astype(np.int64) & 4095) >= W): bad.append("column numbers in br")
    return bad
def reference(res, cap, br, wt, ka):
    R = res.astype(np.float32).astype(np.int32).reshape(N, 8, 16, W); C = cap.astype(np.float32).astype(np.int32).reshape(N, 8, 16, V)
    b = np.array(br, dtype=np.int32).reshape(N, 8, 16, V); w = wt.astype(np.int64).reshape(N, 8, 16, 1); kf = ka.astype(np.int64).reshape(N, 8, 16, 1)
    A = [0] * N; row = np.arange(16).reshape(1, 16, 1); i = np.arange(Q)
    for t in range(1, RO + 1):
        v = S * i + (t - 1) % S; sent = []
        for r in range(N):
            x = b[r][:, :, v]; on = (((x >> 12) & 15) >= t) & (-(x >> 16) < t)
            c = C[r][:, :, v]; most = 4 + (A[r] & 1)
            pick = np.take_along_axis(R[r], (x & 4095).reshape(8, 1, 16 * Q), 2).reshape(8, 16, 16, Q) * on[:, None]
            m = np.max(pick, axis=2); fail = np.sum(m > c, axis=1) > most
            over = np.where(on, np.sum(np.maximum(pick - c[:, :, None], 0), axis=1), -1)
            gone = fail[:, None] & (row == np.argmax(over, axis=1)[:, None])
            m = np.max(pick * (~gone)[:, None], axis=2)
            m = np.where((np.sum(m > c, axis=1) > most)[:, None], 0, m)
            b[r][:, :, v] = np.where(gone, (x & 65535) - 65536 * (t + S), x)
            R[r][:, :, v] = m; A[r] = int(np.sum(fail)); sent.append(m)
        for r in range(N):
            m = sent[(r - 1 - (t - 1) % (N - 1)) % N]
            u = (np.sum(w[r] * m, axis=1) + 37 * i) & 4095
            p = ((u * u >> 5)[:, None] + kf[r] * u[:, None]) & (V - 1)
            slack = np.maximum(C[r] - R[r][:, :, :V], 0)
            sl = np.take_along_axis(slack, p.reshape(8, 1, 16 * Q), 2).reshape(8, 16, 16, Q)
            score = np.sum(np.minimum(m[:, :, None], sl), axis=1)
            par = np.take_along_axis(p, np.argmax(score, axis=1)[:, None], 1)[:, 0]
            for g in range(8):
                node, first = np.unique(par[g], return_index=True)
                b[r, g, first & 15, node] = V + Q * (t - 1) + first + 4096 * (t + 2)
            if t < RO: R[r][:, :, V + Q * (t - 1):V + Q * t] = m
    return {"yr": np.ascontiguousarray(R[..., :V]).reshape(N, 128, V).astype(np.float32).astype(BF), "yb": b.reshape(N, 128, V).astype(np.float32)}

@@ -1,0 +1,464 @@
+from concourse.mybir import AluOpType as A, ActivationFunctionType as F
+
+NT = 6
+Q = 256
+ZC = 3328
+TR = 4128
+MAGIC = 12582912.0
+SCRATCH = {
+    "RES": ("sbuf", [128, 3344], "bfloat16"),
+    "WD": ("sbuf", [128, 2304], "float32"),
+    "BRI": ("sbuf", [128, 2048], "int32"),
+    "PK": ("sbuf", [128, 4384], "bfloat16"),
+    "EQ": ("sbuf", [128, 16, 256], "bfloat16"),
+    "TRI": ("sbuf", [128, 16, 16], "bfloat16"),
+    "SND": ("sbuf", [128, NT * Q], "bfloat16"),
+    "LAND": ("sbuf", [128, NT * Q], "bfloat16"),
+    "D16": ("sbuf", [128, 144], "bfloat16"),
+    "D32": ("sbuf", [128, 144], "bfloat16"),
+    "SW0": ("sbuf", [128, 160], "bfloat16"),
+    "SW1": ("sbuf", [128, 160], "bfloat16"),
+    "IO256": ("sbuf", [128, 16], "bfloat16"),
+    "XB": ("sbuf", [128, 16], "bfloat16"),
+    "HB": ("sbuf", [128, 32], "bfloat16"),
+    "HL": ("sbuf", [128, 32], "int32"),
+    "XK": ("sbuf", [128, 8], "float32"),
+}
+for _n in ("FB", "CM", "CX0", "CX1", "MX", "SC", "SEG", "SP"):
+    SCRATCH[_n] = ("sbuf", [128, 4096], "bfloat16")
+for _n in ("CAP", "SL"):
+    SCRATCH[_n] = ("sbuf", [128, 2048], "bfloat16")
+for _n in ("CC", "P0", "ZER", "ONES", "IOBF", "OFFD", "CMP1", "CMP2", "M1", "M2", "SGN", "DELB", "DELI", "N12", "N16", "N16B", "BD1", "BD2", "NEB", "R1"):
+    SCRATCH[_n] = ("sbuf", [128, 256], "bfloat16")
+for _n in ("IOT", "IO16", "NDEL", "NEW", "MB", "RM", "OFS", "KT", "KSC", "KRV", "KB", "KEY", "VS", "CNS", "WOLD", "FA", "FM"):
+    SCRATCH[_n] = ("sbuf", [128, 256], "float32")
+for _n in ("BO", "NBO", "BO4", "WTL", "ID", "NID", "N20", "IDT", "C37", "KC", "KC2", "KR16", "NEG", "FOUR", "LIMT"):
+    SCRATCH[_n] = ("sbuf", [128, 128], "bfloat16")
+for _n in ("IOB", "PAR"):
+    SCRATCH[_n] = ("sbuf", [128, 128], "float32")
+for _n in ("UI", "UU", "SQ", "PI2"):
+    SCRATCH[_n] = ("sbuf", [128, 256], "int32")
+for _n in ("EO", "P16", "VB", "OFFC"):
+    SCRATCH[_n] = ("sbuf", [128, 256], "uint16")
+for _n in ("WTI", "KAI", "PI", "KI", "HI"):
+    SCRATCH[_n] = ("sbuf", [128, 1], "int32")
+for _n in ("WTF", "KAF", "PF", "KF", "G16", "G15", "P16F", "H0", "H1", "SACC", "PA", "PB", "PC", "ODD"):
+    SCRATCH[_n] = ("sbuf", [128, 1], "float32")
+for _n in ("IL", "TP", "TW", "LX", "LW", "LB", "LC"):
+    SCRATCH[_n] = ("sbuf", [128, 16], "float32")
+for _n in ("XI", "XI2"):
+    SCRATCH[_n] = ("sbuf", [128, 16], "int32")
+for _n in ("KL", "PL", "PW"):
+    SCRATCH[_n] = ("sbuf", [128, 16], "uint16")
+for _n in range(8):
+    SCRATCH["B%d" % _n] = ("psum", [128, 512], "float32")
+SEMAPHORES = ["cv", "ct", "ca", "cp", "dbr", "dres", "dcap", "dwt", "dka", "dtri", "dyr", "dyb", "loc"] + ["arr%d" % t for t in range(1, NT + 1)]
+
+
+def rank_program(g, core, T, topo):
+    rank = T.rank_of(core)
+    if rank is None:
+        return
+    cores = T.cores
+    n = len(cores)
+    queues = {"v": g.vector, "t": g.tensor, "a": g.scalar, "p": g, "s": g.sync}
+    own = {"v": "cv", "t": "ct", "a": "ca", "p": "cp"}
+    count = {k: 0 for k in ("v", "t", "a", "p")}
+    known = {k: {} for k in queues}
+    lastw, readers, banks = {}, {}, {}
+
+    def wait_for(eng, toks):
+        best = {}
+        for tok in toks:
+            if tok[0] not in best or best[tok[0]][1] < tok[1]:
+                best[tok[0]] = tok
+        kn = known[eng]
+        for s, val, snap in sorted(best.values(), key=lambda x: -len(x[2])):
+            if kn.get(s, 0) >= val:
+                continue
+            queues[eng].wait_ge(T.sem[s], val)
+            kn[s] = val
+            for s2, v2 in snap.items():
+                if kn.get(s2, 0) < v2:
+                    kn[s2] = v2
+
+    def banks_of(r, w):
+        return set(x.split(".")[0] for x in list(r) + list(w) if "." in x)
+
+    def deps(eng, r, w):
+        toks = []
+        for k in r:
+            if k in lastw:
+                toks.append(lastw[k])
+        for k in w:
+            if k in lastw:
+                toks.append(lastw[k])
+            toks += list(readers.get(k, {}).values())
+        for k in banks_of(r, w):
+            toks += [tok for e, tok in banks.get(k, {}).items() if e != eng]
+        if eng == "t":
+            toks = [x for x in toks if x[0] != "ct"]
+        return toks
+
+    def note(eng, tok, r, w):
+        for k in r:
+            readers.setdefault(k, {})[tok[0]] = tok
+        for k in w:
+            lastw[k] = tok
+            readers[k] = {}
+        for k in banks_of(r, w):
+            banks.setdefault(k, {})[eng] = tok
+
+    def op(eng, f, r, w):
+        wait_for(eng, deps(eng, r, w))
+        count[eng] += 1
+        tok = (own[eng], count[eng], dict(known[eng]))
+        f().then_inc(T.sem[own[eng]], 1)
+        note(eng, tok, r, w)
+
+    def dma(eng, out, in_, sem, r, w):
+        wait_for(eng, deps(eng, r, w))
+        queues[eng].dma_start(out, in_).then_inc(T.sem[sem], 16)
+        note(eng, (sem, 16, dict(known[eng])), r, w)
+
+    V, PE, AC = g.vector, g.tensor, g.scalar
+
+    def v(f, r, w):
+        op("v", f, r, w)
+
+    def mm(out, lhs, rhs, st, sp, r, w):
+        op("t", lambda: PE.matmul(out, lhs, rhs, st, sp), r, w)
+
+    def act(out, in_, r, w, func=F.Copy, bias=0.0, scale=1.0):
+        op("a", lambda: AC.activation(out, in_, func, bias=bias, scale=scale), r, w)
+
+    def fill(ap, c, k):
+        v(lambda: V.memset(ap, c), [], [k])
+
+    def pfill(ap, c, k, cols):
+        op("p", lambda: g.iota(ap, [[0, cols]], c, 0, allow_small_or_imprecise_dtypes=True), [], [k])
+
+    def ts(out, in0, s1, s2, o0, o1, r, w):
+        if o1 is None:
+            v(lambda: V.tensor_scalar(out, in0, s1, None, o0), r, w)
+        else:
+            v(lambda: V.tensor_scalar(out, in0, s1, s2, o0, o1), r, w)
+
+    def tt(out, a, b, o, r, w):
+        v(lambda: V.tensor_tensor(out, a, b, o), r, w)
+
+    def cp(out, a, r, w):
+        v(lambda: V.tensor_copy(out, a), r, w)
+
+    def scan(out, d0, d1, o0, o1, r, w):
+        v(lambda: V.tensor_tensor_scan(out, d0, d1, 0.0, o0, o1), r, w)
+
+    dma("s", T.BRI[:], T.br[:], "dbr", [], ["BRI"])
+    dma("a", T.RES[:, 0:ZC], T.res[:], "dres", [], ["RES"])
+    dma("s", T.CAP[:], T.cap[:], "dcap", [], ["CAP"])
+    dma("s", T.WTI[:], T.wt[:], "dwt", [], ["WTI"])
+    dma("s", T.KAI[:], T.ka[:], "dka", [], ["KAI"])
+    op("p", lambda: g.iota(T.PI[:], [[0, 1]], 0, 1), [], ["PI"])
+    op("p", lambda: g.iota(T.IOT[:], [[1, 256]], 0, 0, allow_small_or_imprecise_dtypes=True), [], ["IOT"])
+    op("p", lambda: g.iota(T.IO16[:], [[0, 16], [1, 16]], 0, 0, allow_small_or_imprecise_dtypes=True), [], ["IO16"])
+    op("p", lambda: g.iota(T.IOB[:], [[16, 8], [0, 16]], 0, 0, allow_small_or_imprecise_dtypes=True), [], ["IOB"])
+    pfill(T.SP[:], 0, "SP", 4096)
+    pfill(T.ONES[:], 1, "ONES", 256)
+    pfill(T.LIMT[:], 18, "LIMT", 128)
+    pfill(T.ZER[:], 0, "ZER", 256)
+    pfill(T.VS[:], 0, "VS", 256)
+    pfill(T.PAR[:], 1, "PAR", 128)
+    pfill(T.FOUR[:], 4, "FOUR", 128)
+    pfill(T.C37[:], 37, "C37", 128)
+    pfill(T.NEG[:], -131072, "NEG", 128)
+    fill(T.RES[:, ZC:ZC + 16], 0.0, "RESZ")
+    fill(T.SEG[:], 1.0, "SEG")
+    fill(T.SEG[:, 0:4096:16], 0.0, "SEG")
+    fill(T.MB[:], 1e9, "MB")
+    fill(T.MB[:, 0:256:16], -1e9, "MB")
+    fill(T.RM[:], 1.0, "RM")
+    fill(T.RM[:, 15:256:16], 0.0, "RM")
+    act(T.KC[:], T.IO16[:, 0:128], ["IO16"], ["KC"], bias=15.0, scale=-1.0)
+    act(T.KC2[:], T.IO16[:, 0:128], ["IO16"], ["KC2"], bias=30720.0, scale=-2048.0)
+    act(T.KR16[:], T.IO16[:, 0:128], ["IO16"], ["KR16"], scale=16.0)
+    act(T.IO256[:], T.IOT[:, 0:16], ["IOT"], ["IO256"], scale=256.0)
+    act(T.IOBF[:], T.IOT[:], ["IOT"], ["IOBF"])
+    ts(T.KI[:], T.PI[:], 15, None, A.bitwise_and, None, ["PI"], ["KI"])
+    ts(T.HI[:], T.PI[:], 16, None, A.bitwise_and, None, ["PI"], ["HI"])
+    cp(T.PF[:], T.PI[:], ["PI"], ["PF"])
+    cp(T.KF[:], T.KI[:], ["KI"], ["KF"])
+    tt(T.G16[:], T.PF[:], T.KF[:], A.subtract, ["PF", "KF"], ["G16"])
+    ts(T.G15[:], T.G16[:], 15.0, None, A.add, None, ["G16"], ["G15"])
+    ts(T.P16F[:], T.PF[:], 16.0, None, A.add, None, ["PF"], ["P16F"])
+    ts(T.H1[:], T.HI[:], 0.0625, None, A.mult, None, ["HI"], ["H1"])
+    ts(T.H0[:], T.HI[:], -0.0625, 1.0, A.mult, A.add, ["HI"], ["H0"])
+    ts(T.D16[:], T.IOT[:, 0:144], T.G15[:, 0:1], 16.0, A.is_equal, A.mult, ["IOT", "G15"], ["D16"])
+    ts(T.NBO[:], T.IOB[:], T.G16[:, 0:1], -512.0, A.is_equal, A.mult, ["IOB", "G16"], ["NBO"])
+
+    def one_hot(out, off, pos, value, r, w):
+        if value is None:
+            ts(out, off, pos, None, A.is_equal, None, r, w)
+        else:
+            ts(out, off, pos, value, A.is_equal, A.mult, r, w)
+
+    def more_constants():
+        one_hot(T.ID[:], T.IOT[:, 0:128], T.PF[:, 0:1], None, ["IOT", "PF"], ["ID"])
+        one_hot(T.NID[:], T.IOT[:, 0:128], T.PF[:, 0:1], -1.0, ["IOT", "PF"], ["NID"])
+        one_hot(T.N20[:], T.IOT[:, 0:128], T.PF[:, 0:1], -1048576.0, ["IOT", "PF"], ["N20"])
+        one_hot(T.BO[:], T.IOB[:], T.G16[:, 0:1], None, ["IOB", "G16"], ["BO"])
+        one_hot(T.BO4[:], T.IOB[:], T.G16[:, 0:1], 8192.0, ["IOB", "G16"], ["BO4"])
+        one_hot(T.D32[:], T.IOT[:, 0:144], T.G15[:, 0:1], 32768.0, ["IOT", "G15"], ["D32"])
+        one_hot(T.SW0[:], T.IOT[:, 0:160], T.P16F[:, 0:1], T.H0[:, 0:1], ["IOT", "P16F", "H0"], ["SW0"])
+        one_hot(T.SW1[:], T.IOT[:, 0:160], T.P16F[:, 0:1], T.H1[:, 0:1], ["IOT", "P16F", "H1"], ["SW1"])
+        one_hot(T.DELB[:], T.IO16[:], T.KF[:, 0:1], None, ["IO16", "KF"], ["DELB"])
+        ts(T.NDEL[:], T.IO16[:], T.KF[:, 0:1], None, A.not_equal, None, ["IO16", "KF"], ["NDEL"])
+        ts(T.OFFD[:], T.IO16[:], T.KF[:, 0:1], -2097152.0, A.not_equal, A.mult, ["IO16", "KF"], ["OFFD"])
+        ts(T.M2[:], T.IO16[:], T.KF[:, 0:1], None, A.is_gt, None, ["IO16", "KF"], ["M2"])
+        dma("s", T.TRI[:], T.M2[:], "dtri", ["M2"], ["TRI"])
+        tt(T.DELI[:], T.IOT[:], T.DELB[:], A.mult, ["IOT", "DELB"], ["DELI"])
+        cp(T.OFFC[:], T.IOT[:], ["IOT"], ["OFFC"])
+
+    def last_constants():
+        cp(T.WTF[:], T.WTI[:], ["WTI"], ["WTF"])
+        cp(T.KAF[:], T.KAI[:], ["KAI"], ["KAF"])
+        ts(T.WTL[:], T.BO[:], T.WTF[:, 0:1], None, A.mult, None, ["BO", "WTF"], ["WTL"])
+        ts(T.IL[:], T.IOT[:, 0:16], 16.0, T.KF[:, 0:1], A.mult, A.add, ["IOT", "KF"], ["IL"])
+        ts(T.TP[:], T.IL[:], float(TR), None, A.add, None, ["IL"], ["TP"])
+        ts(T.TW[:], T.IL[:], 2048.0, None, A.add, None, ["IL"], ["TW"])
+        ts(T.XK[:], T.IOT[:, 0:8], -2.0, T.KF[:, 0:1], A.mult, A.add, ["IOT", "KF"], ["XK"])
+
+    def floors(src, size, out, ok, sign):
+        act(T.FA[:], src, ["WD"], ["FA"], bias=-0.5 + 0.5 / size, scale=1.0 / size)
+        act(T.FM[:], T.FA[:], ["FA"], ["FM"], bias=MAGIC)
+        act(out, T.FM[:], ["FM"], [ok], bias=-sign * size * MAGIC, scale=sign * size)
+
+    def first_offsets():
+        src = T.BRI[:, 0:2048:8]
+        ts(T.OFS[:], src, 0.0, 4096.0, A.is_lt, A.mult, ["BRI"], ["OFS"])
+        ts(T.UU[:], src, 65535, None, A.bitwise_and, None, ["BRI"], ["UU"])
+        ts(T.UI[:], src, 4095, None, A.bitwise_and, None, ["BRI"], ["UI"])
+        ts(T.KT[:], T.UU[:], 4096.0, 4096.0, A.is_lt, A.mult, ["UU"], ["KT"])
+        tt(T.OFS[:], T.OFS[:], T.KT[:], A.max, ["OFS", "KT"], ["OFS"])
+        tt(T.OFS[:], T.OFS[:], T.UI[:], A.max, ["OFS", "UI"], ["OFS"])
+        ts(T.EO[:], T.OFS[:], float(ZC), None, A.min, None, ["OFS"], ["EO"])
+
+    def offsets_a(t):
+        w = T.WD[:, t - 1:2048:8]
+        floors(w, 4096.0, T.N12[:], "N12", 1.0)
+        floors(w, 65536.0, T.N16[:], "N16", -1.0)
+        act(T.BD2[:], T.N16[:], ["N16"], ["BD2"], F.Relu, bias=-65536.0 * (t - 1))
+
+    def offsets_b(t):
+        mm(T.B6[:, 256:512], T.ID[:], T.N12[:], True, False, ["ID", "N12"], ["B6.t"])
+        mm(T.B6[:, 256:512], T.ID[:], T.N16[:], False, True, ["ID", "N16"], ["B6.t"])
+        act(T.BD1[:], T.B6[:, 256:512], ["B6.t"], ["BD1"], F.Relu, bias=4096.0 * t, scale=-1.0)
+        mm(T.B2[:, 256:512], T.NID[:], T.N12[:], True, False, ["NID", "N12"], ["B2.off"])
+        mm(T.B2[:, 256:512], T.ID[:], T.BD1[:], False, False, ["ID", "BD1"], ["B2.off"])
+        mm(T.B2[:, 256:512], T.ID[:], T.BD2[:], False, True, ["ID", "BD2"], ["B2.off"])
+
+    def offsets_c(t):
+        tt(T.OFS[:], T.WD[:, t - 1:2048:8], T.B2[:, 256:512], A.add, ["WD", "B2.off"], ["OFS"])
+        ts(T.EO[:], T.OFS[:], float(ZC), None, A.min, None, ["OFS"], ["EO"])
+
+    def bulk():
+        act(T.PK[:, 0:4096], T.RES[:, 0:3344].indirect(T.EO[:, 0:256]), ["RES", "RESZ", "EO"], ["PK"])
+
+    def cap_room(t):
+        act(T.B0[:, 0:256], T.CAP[:, t - 1:2048:8], ["CAP"], ["B0.cap"])
+
+    def cap_wide(t):
+        act(T.CC[:], T.CAP[:, t - 1:2048:8], ["CAP"], ["CC"])
+        act(T["CX%d" % (t & 1)][:], T.CC[:].indirect(T.OFFC[:, 0:256]), ["CC", "OFFC"], ["CX%d" % (t & 1)])
+
+    def to_list(col, key, parts, wkey, first):
+        for ip in (0, 1):
+            for h in (0, 1):
+                sw, o = (T.SW0, (16, 0)[h]) if ip == 0 else (T.SW1, (32, 16)[h])
+                for j, p in enumerate(parts):
+                    mm(T.B4[:, col + ip:col + 16:2], sw[:, o:o + 128], p[:, h:16:2], first and h == 0 and j == 0,
+                       (first or ip == 1) and h == 1 and j == len(parts) - 1, ["SW0", "SW1", key], [wkey])
+
+    def set_words():
+        tt(T.WOLD[:], T.WD[:, 0:2304].indirect(T.PW[:, 0:16]), T.NDEL[:], A.mult, ["WD", "PW", "NDEL"], ["WOLD"])
+        tt(T.WD[:, 0:2304].indirect(T.PW[:, 0:16]), T.WOLD[:], T.NEW[:], A.add, ["WOLD", "NEW", "PW"], ["WD"])
+
+    def suspended(t):
+        tt(T.WD[:, t - 1:2048:8], T.WD[:, t - 1:2048:8], T.B3[:, 256:512], A.subtract, ["WD", "B3.z"], ["WD"])
+
+    def parity():
+        op("a", lambda: AC.activation(T.SGN[:], T.B2[:, 0:256], F.Sign, accum_out=T.SACC[:]), ["B2.c1"], ["SGN", "SACC"])
+        mm(T.B5[:, 0:1], T.PAR[:], T.SACC[:], True, True, ["PAR", "SACC"], ["B5.par"])
+        act(T.PA[:], T.B5[:, 0:1], ["B5.par"], ["PA"], scale=-0.03125)
+        act(T.PB[:], T.PA[:], ["PA"], ["PB"], bias=-0.25, scale=0.5)
+        act(T.PC[:], T.PB[:], ["PB"], ["PC"], bias=MAGIC)
+        act(T.PB[:], T.PC[:], ["PC"], ["PB"], bias=2.0 * MAGIC, scale=-2.0)
+        op("a", lambda: AC.activation(T.ODD[:], T.PB[:], F.Identity, bias=T.PA[:, 0:1]), ["PA", "PB"], ["ODD"])
+
+    def new_words():
+        mm(T.B7[:, 256:512], T.ID[:], T.DELI[:], True, False, ["ID", "DELI"], ["B7.n"])
+        mm(T.B7[:, 256:512], T.IDT[:], T.DELB[:], False, True, ["IDT", "DELB"], ["B7.n"])
+        act(T.NEW[:], T.B7[:, 256:512], ["B7.n"], ["NEW"])
+
+    more_constants()
+    first_offsets()
+    act(T.PK[:, 0:3072], T.RES[:, 0:3344].indirect(T.EO[:, 0:192]), ["RES", "RESZ", "EO"], ["PK"])
+    cap_room(1)
+    cp(T.SP[:, 0:4096:16], T.CAP[:, 0:2048:8], ["CAP"], ["SP"])
+    scan(T.CX1[:], T.SEG[:], T.SP[:], A.mult, A.max, ["SEG", "SP"], ["CX1"])
+    cp(T.PK[:, 3072:4096], T.RES[:, 0:3344].indirect(T.EO[:, 192:256]), ["RES", "RESZ", "EO"], ["PKx"])
+    last_constants()
+    for j in range(4):
+        b, k = (T.B5, "B5.x") if j % 2 else (T.B7, "B7.x")
+        s = slice(512 * j, 512 * j + 512)
+        mm(b[:], T.ID[:], T.CAP[:, s], True, False, ["ID", "CAP"], [k])
+        mm(b[:], T.NID[:], T.RES[:, s], False, True, ["NID", "RES"], [k])
+        act(T.SL[:, s], b[:], [k], ["SL"], F.Relu)
+
+    for t in range(1, NT + 1):
+        c = t - 1
+        cx = "CX%d" % (t & 1)
+        L0 = c * Q
+        land, lk = T.LAND[:, L0:L0 + Q], "LAND%d" % t
+        snd, sk = T.SND[:, L0:L0 + Q], "SND%d" % t
+        cp(T.P0[:], T.PK[:, 0:4096:16], ["PK", "PKx"], ["P0"])
+        v(lambda: V.memset(T.PK[:, 0:4096:16], 255.0), [], ["PK"])
+        mm(T.B1[:, 0:256], T.KC[0:1, :], T.ONES[0:1, :], True, False, ["KC", "ONES"], ["B1.ks"])
+        for j in range(4):
+            s = slice(1024 * j, 1024 * j + 1024)
+            scan(T.CM[:, s], T[cx][:, s], T.PK[:, s], A.min, A.max, [cx, "PK"], ["CM%d" % j])
+            tt(T.CM[:, 1024 * j:1024 * j + 1024:16], T.P0[:, 64 * j:64 * j + 64], T.B0[:, 64 * j:64 * j + 64], A.max, ["P0", "B0.cap"], ["CM%d" % j])
+            for k in range(16):
+                mm(T.B1[:, 64 * j:64 * j + 64], T.D16[:, 15 - k:143 - k], T.CM[:, 1024 * j + k:1024 * j + 1024:16], False, j == 3 and k == 15,
+                   ["D16", "CM%d" % j], ["B1.ks"])
+        cp(T.PK[:, 0:4096:16], T.P0[:], ["P0"], ["PK"])
+        if 1 < t < NT:
+            cap_wide(t + 1)
+        if t > 1:
+            set_words()
+        else:
+            cp(T.WD[:, 0:2048], T.BRI[:], ["BRI"], ["WD"])
+            fill(T.WD[:, 2048:2304], 0.0, "WD")
+        if t < NT:
+            offsets_a(t + 1)
+        floors(T.WD[:, c:2048:8], 65536.0, T.N16B[:], "N16B", -1.0)
+        act(T.IDT[:], T.ID[:], ["ID"], ["IDT"], scale=2048.0 + 256.0 * c + 4096.0 * (t + 2))
+        scan(T.FB[:], T.SEG[:], T.PK[:, 0:4096], A.mult, A.max, ["SEG", "PK"], ["FB"])
+        tt(T.CMP1[:], T.FB[:, 15:4096:16], T.B0[:, 0:256], A.is_gt, ["FB", "B0.cap"], ["CMP1"])
+        mm(T.B2[:, 0:256], T.LIMT[:], T.ONES[:], True, False, ["LIMT", "ONES"], ["B2.c1"])
+        mm(T.B2[:, 0:256], T.NBO[:], T.CMP1[:], False, True, ["NBO", "CMP1"], ["B2.c1"])
+        mm(T.B4[:, 0:16], T.KR16[0:1, :], T.ONES[0:1, 0:16], True, False, ["KR16", "ONES"], ["B4.kl"])
+        mm(T.B4[:, 0:16], T.ONES[0:1, 0:128], T.IO256[0:1, :], False, False, ["IO256", "ONES"], ["B4.kl"])
+        v(lambda: V.transpose(T.KT[:], T.B1[:, 0:256]), ["B1.ks"], ["KT"])
+        scan(T.KSC[:], T.MB[:], T.KT[:], A.min, A.max, ["MB", "KT"], ["KSC"])
+        cp(T.XI[:], T.KSC[:, 15:256:16], ["KSC"], ["XI"])
+        ts(T.XI2[:], T.XI[:], 15, None, A.bitwise_and, None, ["XI"], ["XI2"])
+        ts(T.XB[:], T.XI2[:], -1.0, 15.0, A.mult, A.add, ["XI2"], ["XB"])
+        to_list(0, "XB", [T.XB], "B4.kl", False)
+        tt(T.M1[:], T.FB[:, 15:4096:16], T.B2[:, 0:256], A.min, ["FB", "B2.c1"], ["M1"])
+        ts(T.B0[:, 256:512], T.M1[:], 0.0, None, A.max, None, ["M1"], ["B0.m1"])
+        if t < NT:
+            offsets_b(t + 1)
+        new_words()
+        act(T.R1[:], T.B2[:, 0:256], ["B2.c1"], ["R1"], F.Relu, scale=4096.0)
+        if t < NT:
+            parity()
+        cp(T.KL[:], T.B4[:, 0:16], ["B4.kl"], ["KL"])
+        v(lambda: V.tensor_copy(T.PK[:, 0:4096].indirect(T.KL[:, 0:16]), T.ZER[:]), ["KL", "ZER"], ["PK"])
+        scan(T.FB[:], T.SEG[:], T.PK[:, 0:4096], A.mult, A.max, ["SEG", "PK"], ["FB"])
+        tt(T.CMP2[:], T.FB[:, 15:4096:16], T.B0[:, 0:256], A.is_gt, ["FB", "B0.cap"], ["CMP2"])
+        mm(T.B3[:, 0:256], T.LIMT[:], T.ONES[:], True, False, ["LIMT", "ONES"], ["B3.c2"])
+        mm(T.B3[:, 0:256], T.NBO[:], T.CMP2[:], False, True, ["NBO", "CMP2"], ["B3.c2"])
+        tt(T.M2[:], T.FB[:, 15:4096:16], T.B3[:, 0:256], A.min, ["FB", "B3.c2"], ["M2"])
+        tt(snd, T.M2[:], T.B0[:, 256:512], A.max, ["M2", "B0.m1"], [sk])
+        dst = cores[(rank + 1 + c % (n - 1)) % n]
+        rid, pid, _s = topo.addr(dst)
+        wait_for("p", deps("p", [sk], []))
+        g.remote_dma(land, snd, T.sem["arr%d" % t], T.sem.loc, pid, rid, topo.mask(core, dst))
+        lastw[lk] = ("arr%d" % t, len(topo.engines(core, dst)), {})
+        mm(T.B5[:, 256:512], T.ID[:], T.CAP[:, c:2048:8], True, False, ["ID", "CAP"], ["B5.sl"])
+        mm(T.B5[:, 256:512], T.NID[:], snd, False, True, ["NID", sk], ["B5.sl"])
+        act(T.SL[:, c:2048:8], T.B5[:, 256:512], ["B5.sl"], ["SL"], F.Relu)
+        act(T.RES[:, c:2048:8], snd, [sk], ["RES"])
+        if t == NT:
+            dma("s", T.yr[:], T.RES[:, 0:2048], "dyr", ["RES"], ["yr"])
+        if t < NT:
+            cap_room(t + 1)
+            op("a", lambda: AC.activation(T.LIMT[:], T.FOUR[:], F.Copy, bias=18.0, scale=T.ODD[:, 0:1]), ["FOUR", "ODD"], ["LIMT"])
+        scan(T.KRV[:, ::-1], T.RM[:, ::-1], T.KSC[:, ::-1], A.mult, A.max, ["RM", "KSC"], ["KRV"])
+        v(lambda: V.transpose(T.KB[:], T.KRV[:]), ["KRV"], ["KB"])
+        tt(T.NEB[:], T.B1[:, 0:256], T.KB[:], A.not_equal, ["B1.ks", "KB"], ["NEB"])
+        if t < NT:
+            offsets_c(t + 1)
+        mm(T.B5[:, 0:256], T.C37[0:1, :], T.IOBF[0:1, :], True, False, ["C37", "IOBF"], ["B5.u"])
+        mm(T.B5[:, 0:256], T.WTL[:], land, False, True, ["WTL", lk], ["B5.u"])
+        for j in range(4):
+            act(T.MX[:, 1024 * j:1024 * j + 1024], land.indirect(T.OFFC[:, 64 * j:64 * j + 64]), [lk, "OFFC"], ["MX%d" % j])
+        mm(T.B3[:, 256:512], T.NID[:], T.N16B[:], True, False, ["NID", "N16B"], ["B3.z"])
+        mm(T.B3[:, 256:512], T.N20[:], T.NEB[:], False, False, ["N20", "NEB"], ["B3.z"])
+        mm(T.B3[:, 256:512], T.NID[:], T.R1[:], False, True, ["NID", "R1"], ["B3.z"])
+        cp(T.UI[:], T.B5[:, 0:256], ["B5.u"], ["UI"])
+        ts(T.UU[:], T.UI[:], 4095, None, A.bitwise_and, None, ["UI"], ["UU"])
+        ts(T.B5[:, 256:512], T.UU[:], T.KAF[:, 0:1], None, A.mult, None, ["UU", "KAF"], ["B5.fu"])
+        tt(T.SQ[:], T.UU[:], T.UU[:], A.mult, ["UU"], ["SQ"])
+        ts(T.SQ[:], T.SQ[:], 5, None, A.arith_shift_right, None, ["SQ"], ["SQ"])
+        tt(T.PI2[:], T.SQ[:], T.B5[:, 256:512], A.add, ["SQ", "B5.fu"], ["PI2"])
+        ts(T.PI2[:], T.PI2[:], 2047, None, A.bitwise_and, None, ["PI2"], ["PI2"])
+        cp(T.P16[:], T.PI2[:], ["PI2"], ["P16"])
+        act(T.B3[:, 256:512], T.B3[:, 256:512], ["B3.z"], ["B3.z"], F.Relu, bias=65536.0 * (t + 8))
+        if t < NT:
+            act(T.RES[:, 2048 + L0:2048 + L0 + Q], land, [lk], ["RES"])
+            bulk()
+        if t == 1:
+            cap_wide(2)
+        mm(T.B6[:, 0:256], T.NEG[:], T.ONES[:], True, False, ["NEG", "ONES"], ["B6.x"])
+        mm(T.B6[:, 0:256], T.KC2[0:1, :], T.ONES[0:1, :], False, False, ["KC2", "ONES"], ["B6.x"])
+        for j in range(4):
+            s = slice(1024 * j, 1024 * j + 1024)
+            tt(T.SC[:, s], T.SL[:, 0:2048].indirect(T.P16[:, 64 * j:64 * j + 64]), T.MX[:, s], A.min, ["SL", "P16", "MX%d" % j], ["SC%d" % j])
+            for k in range(16):
+                mm(T.B6[:, 64 * j:64 * j + 64], T.D32[:, 15 - k:143 - k], T.SC[:, 1024 * j + k:1024 * j + 1024:16], False, j == 3 and k == 15,
+                   ["D32", "SC%d" % j], ["B6.x"])
+        mm(T.B7[:, 0:256], T.ID[:], T.OFFD[:], True, False, ["ID", "OFFD"], ["B7.x"])
+        suspended(t)
+        tt(T.KEY[:], T.B6[:, 0:256], T.PI2[:], A.add, ["B6.x", "PI2"], ["KEY"])
+        v(lambda: V.transpose(T.KT[:], T.KEY[:]), ["KEY"], ["KT"])
+        scan(T.KSC[:], T.MB[:], T.KT[:], A.min, A.max, ["MB", "KT"], ["KSC"])
+        cp(T.XI[:], T.KSC[:, 15:256:16], ["KSC"], ["XI"])
+        ts(T.HL[:, 0:16], T.XI[:], 2040, None, A.bitwise_and, None, ["XI"], ["HLa"])
+        ts(T.HL[:, 16:32], T.XI[:], 7, None, A.bitwise_and, None, ["XI"], ["HLb"])
+        cp(T.HB[:], T.HL[:], ["HLa", "HLb"], ["HB"])
+        to_list(32, "HB", [T.HB, T.HB[:, 16:32]], "B4.lv", True)
+        to_list(48, "HB", [T.HB[:, 16:32]], "B4.lv", True)
+        tt(T.VS[:, 15:256:16], T.HL[:, 0:16], T.HL[:, 16:32], A.add, ["HLa", "HLb"], ["VS"])
+        scan(T.KRV[:, ::-1], T.RM[:, ::-1], T.VS[:, ::-1], A.mult, A.max, ["RM", "VS"], ["KRV"])
+        v(lambda: V.transpose(T.KB[:], T.KRV[:]), ["KRV"], ["KB"])
+        cp(T.VB[:], T.KB[:], ["KB"], ["VB"])
+        for q in range(2):
+            for i in range(8 * q, 8 * q + 8):
+                ts(T.EQ[:, i, 0:256 - 16 * i], T.VB[:, 16 * i:256], T.B4[:, 32 + i:33 + i], None, A.is_equal, None, ["VB", "B4.lv"], ["EQ%d" % q])
+            tt(T.EQ[:, 8 * q:8 * q + 8, 0:16], T.EQ[:, 8 * q:8 * q + 8, 0:16], T.TRI[:, 8 * q:8 * q + 8, :], A.mult, ["EQ%d" % q, "TRI"], ["EQ%d" % q])
+            for i in range(8 * q, 8 * q + 8):
+                mm(T.B7[:, 16 * i:256], T.BO4[:], T.EQ[:, i, 0:256 - 16 * i], False, i == 15, ["BO4", "EQ%d" % q], ["B7.x"])
+        lv = T.B4[:, 32:48]
+        if t < NT:
+            ts(T.LW[:], T.B4[:, 48:64], float(t), 8192.0, A.not_equal, A.mult, ["B4.lv"], ["LW"])
+            ts(T.LX[:], lv, 2.0, T.XK[:, t:t + 1], A.mult, A.add, ["B4.lv", "XK"], ["LX"])
+            tt(T.LW[:], T.LW[:], T.TP[:], A.min, ["LW", "TP"], ["LW"])
+            tt(T.LX[:], T.LW[:], T.LX[:], A.max, ["LW", "LX"], ["LX"])
+        scan(T.CNS[:], T.MB[:], T.B7[:, 0:256], A.min, A.max, ["MB", "B7.x"], ["CNS"])
+        if t < NT:
+            tt(T.LB[:], T.CNS[:, 15:256:16], T.TP[:], A.min, ["CNS", "TP"], ["LB"])
+            tt(T.LC[:], T.LB[:], T.LX[:], A.max, ["LB", "LX"], ["LC"])
+            cp(T.PL[:], T.LC[:], ["LC"], ["PL"])
+            v(lambda: V.tensor_copy(T.PK[:, 0:4384].indirect(T.PL[:, 0:16]), land), ["PL", lk], ["PK"])
+        tt(T.LB[:], T.CNS[:, 15:256:16], T.TW[:], A.min, ["CNS", "TW"], ["LB"])
+        tt(T.LC[:], T.LB[:], lv, A.max, ["LB", "B4.lv"], ["LC"])
+        cp(T.PW[:], T.LC[:], ["LC"], ["PW"])
+
+    set_words()
+    dma("s", T.yb[:], T.WD[:, 0:2048], "dyb", ["WD"], ["yb"])
+    g.wait_ge(T.sem.loc, sum(len(topo.engines(core, cores[(rank + 1 + c % (n - 1)) % n])) for c in range(NT)))
+    for s, k in own.items():
+        g.wait_ge(T.sem[k], count[s])
+    for s in ("dyr", "dyb", "dtri", "dbr", "dres", "dcap", "dwt", "dka"):
+        g.wait_ge(T.sem[s], 16)

@@ -11,7 +11,6 @@ SCRATCH = {
     "BRI": ("sbuf", [128, 2048], "int32"),
     "PK": ("sbuf", [128, 4384], "bfloat16"),
     "EQ": ("sbuf", [128, 16, 256], "bfloat16"),
-    "TRI": ("sbuf", [128, 16, 16], "bfloat16"),
     "SND": ("sbuf", [128, NT * Q], "bfloat16"),
     "LAND": ("sbuf", [128, NT * Q], "bfloat16"),
     "D16": ("sbuf", [128, 144], "bfloat16"),
@@ -28,11 +27,11 @@ for _n in ("FB", "CM", "CX0", "CX1", "MX", "SC", "SEG", "SP"):
     SCRATCH[_n] = ("sbuf", [128, 4096], "bfloat16")
 for _n in ("CAP", "SL"):
     SCRATCH[_n] = ("sbuf", [128, 2048], "bfloat16")
-for _n in ("CC", "P0", "ZER", "ONES", "IOBF", "OFFD", "CMP1", "CMP2", "M1", "M2", "SGN", "DELB", "DELI", "N12", "N16", "N16B", "BD1", "BD2", "NEB", "R1"):
+for _n in ("CC", "P0", "ZER", "ONES", "IOBF", "OFFD", "CMP1", "CMP2", "M1", "M2", "SGN", "DELB", "DELI", "N12", "N16", "N16B", "BD1", "BD2", "NEB", "R0"):
     SCRATCH[_n] = ("sbuf", [128, 256], "bfloat16")
 for _n in ("IOT", "IO16", "NDEL", "NEW", "MB", "RM", "OFS", "KT", "KSC", "KRV", "KB", "KEY", "VS", "CNS", "WOLD", "FA", "FM"):
     SCRATCH[_n] = ("sbuf", [128, 256], "float32")
-for _n in ("BO", "NBO", "BO4", "WTL", "ID", "NID", "N20", "IDT", "C37", "KC", "KC2", "KR16", "NEG", "FOUR", "LIMT"):
+for _n in ("BO", "NBO", "BO4", "BT4", "WTL", "ID", "NID", "N20", "IDT", "C37", "KC", "KC2", "KR16", "NEG", "FOUR", "LIMT"):
     SCRATCH[_n] = ("sbuf", [128, 128], "bfloat16")
 for _n in ("IOB", "PAR"):
     SCRATCH[_n] = ("sbuf", [128, 128], "float32")
@@ -52,7 +51,7 @@ for _n in ("KL", "PL", "PW"):
     SCRATCH[_n] = ("sbuf", [128, 16], "uint16")
 for _n in range(8):
     SCRATCH["B%d" % _n] = ("psum", [128, 512], "float32")
-SEMAPHORES = ["cv", "ct", "ca", "cp", "dbr", "dres", "dcap", "dwt", "dka", "dtri", "dyr", "dyb", "loc"] + ["arr%d" % t for t in range(1, NT + 1)]
+SEMAPHORES = ["cv", "ct", "ca", "cp", "dbr", "dres", "dcap", "dwt", "dka", "dyr", "dyb", "loc"] + ["arr%d" % t for t in range(1, NT + 1)]
 
 
 def rank_program(g, core, T, topo):
@@ -203,29 +202,29 @@ def rank_program(g, core, T, topo):
 
     def more_constants():
         one_hot(T.ID[:], T.IOT[:, 0:128], T.PF[:, 0:1], None, ["IOT", "PF"], ["ID"])
-        one_hot(T.NID[:], T.IOT[:, 0:128], T.PF[:, 0:1], -1.0, ["IOT", "PF"], ["NID"])
-        one_hot(T.N20[:], T.IOT[:, 0:128], T.PF[:, 0:1], -1048576.0, ["IOT", "PF"], ["N20"])
-        one_hot(T.BO[:], T.IOB[:], T.G16[:, 0:1], None, ["IOB", "G16"], ["BO"])
-        one_hot(T.BO4[:], T.IOB[:], T.G16[:, 0:1], 8192.0, ["IOB", "G16"], ["BO4"])
-        one_hot(T.D32[:], T.IOT[:, 0:144], T.G15[:, 0:1], 32768.0, ["IOT", "G15"], ["D32"])
         one_hot(T.SW0[:], T.IOT[:, 0:160], T.P16F[:, 0:1], T.H0[:, 0:1], ["IOT", "P16F", "H0"], ["SW0"])
         one_hot(T.SW1[:], T.IOT[:, 0:160], T.P16F[:, 0:1], T.H1[:, 0:1], ["IOT", "P16F", "H1"], ["SW1"])
         one_hot(T.DELB[:], T.IO16[:], T.KF[:, 0:1], None, ["IO16", "KF"], ["DELB"])
-        ts(T.NDEL[:], T.IO16[:], T.KF[:, 0:1], None, A.not_equal, None, ["IO16", "KF"], ["NDEL"])
-        ts(T.OFFD[:], T.IO16[:], T.KF[:, 0:1], -2097152.0, A.not_equal, A.mult, ["IO16", "KF"], ["OFFD"])
-        ts(T.M2[:], T.IO16[:], T.KF[:, 0:1], None, A.is_gt, None, ["IO16", "KF"], ["M2"])
-        dma("s", T.TRI[:], T.M2[:], "dtri", ["M2"], ["TRI"])
-        tt(T.DELI[:], T.IOT[:], T.DELB[:], A.mult, ["IOT", "DELB"], ["DELI"])
-        cp(T.OFFC[:], T.IOT[:], ["IOT"], ["OFFC"])
+        ts(T.BT4[:], T.IO16[:, 0:128], T.KF[:, 0:1], 8192.0, A.is_gt, A.mult, ["IO16", "KF"], ["BT4"])
+        act(T.BO[:], T.NBO[:], ["NBO"], ["BO"], scale=-0.001953125)
+        act(T.NID[:], T.ID[:], ["ID"], ["NID"], scale=-1.0)
+        act(T.N20[:], T.ID[:], ["ID"], ["N20"], scale=-1048576.0)
+        act(T.BO4[:], T.NBO[:], ["NBO"], ["BO4"], scale=-16.0)
+        act(T.D32[:], T.D16[:], ["D16"], ["D32"], scale=2048.0)
+        act(T.NDEL[:], T.DELB[:], ["DELB"], ["NDEL"], bias=1.0, scale=-1.0)
+        act(T.OFFD[:], T.DELB[:], ["DELB"], ["OFFD"], bias=-2097152.0, scale=2097152.0)
+        op("a", lambda: AC.activation(T.IL[:], T.IOT[:, 0:16], F.Identity, bias=T.KF[:, 0:1], scale=16.0), ["IOT", "KF"], ["IL"])
+        act(T.TP[:], T.IL[:], ["IL"], ["TP"], bias=float(TR))
+        act(T.TW[:], T.IL[:], ["IL"], ["TW"], bias=2048.0)
+        op("a", lambda: AC.activation(T.XK[:], T.IOT[:, 0:8], F.Identity, bias=T.KF[:, 0:1], scale=-2.0), ["IOT", "KF"], ["XK"])
 
     def last_constants():
+        tt(T.BT4[:], T.BT4[:], T.BO[:], A.mult, ["BT4", "BO"], ["BT4"])
+        tt(T.DELI[:], T.IOT[:], T.DELB[:], A.mult, ["IOT", "DELB"], ["DELI"])
+        cp(T.OFFC[:], T.IOT[:], ["IOT"], ["OFFC"])
         cp(T.WTF[:], T.WTI[:], ["WTI"], ["WTF"])
         cp(T.KAF[:], T.KAI[:], ["KAI"], ["KAF"])
         ts(T.WTL[:], T.BO[:], T.WTF[:, 0:1], None, A.mult, None, ["BO", "WTF"], ["WTL"])
-        ts(T.IL[:], T.IOT[:, 0:16], 16.0, T.KF[:, 0:1], A.mult, A.add, ["IOT", "KF"], ["IL"])
-        ts(T.TP[:], T.IL[:], float(TR), None, A.add, None, ["IL"], ["TP"])
-        ts(T.TW[:], T.IL[:], 2048.0, None, A.add, None, ["IL"], ["TW"])
-        ts(T.XK[:], T.IOT[:, 0:8], -2.0, T.KF[:, 0:1], A.mult, A.add, ["IOT", "KF"], ["XK"])
 
     def floors(src, size, out, ok, sign):
         act(T.FA[:], src, ["WD"], ["FA"], bias=-0.5 + 0.5 / size, scale=1.0 / size)
@@ -266,9 +265,11 @@ def rank_program(g, core, T, topo):
     def cap_room(t):
         act(T.B0[:, 0:256], T.CAP[:, t - 1:2048:8], ["CAP"], ["B0.cap"])
 
-    def cap_wide(t):
-        act(T.CC[:], T.CAP[:, t - 1:2048:8], ["CAP"], ["CC"])
-        act(T["CX%d" % (t & 1)][:], T.CC[:].indirect(T.OFFC[:, 0:256]), ["CC", "OFFC"], ["CX%d" % (t & 1)])
+    def cap_wide(t, half):
+        cx = "CX%d" % (t & 1)
+        if half or t == 2:
+            act(T.CC[:], T.CAP[:, t - 1:2048:8], ["CAP"], ["CC"])
+        act(T[cx][:, 2048 * half:2048 * half + 2048], T.CC[:].indirect(T.OFFC[:, 128 * half:128 * half + 128]), ["CC", "OFFC"], ["%s%d" % (cx, half)])
 
     def to_list(col, key, parts, wkey, first):
         for ip in (0, 1):
@@ -304,7 +305,7 @@ def rank_program(g, core, T, topo):
     act(T.PK[:, 0:3072], T.RES[:, 0:3344].indirect(T.EO[:, 0:192]), ["RES", "RESZ", "EO"], ["PK"])
     cap_room(1)
     cp(T.SP[:, 0:4096:16], T.CAP[:, 0:2048:8], ["CAP"], ["SP"])
-    scan(T.CX1[:], T.SEG[:], T.SP[:], A.mult, A.max, ["SEG", "SP"], ["CX1"])
+    scan(T.CX1[:], T.SEG[:], T.SP[:], A.mult, A.max, ["SEG", "SP"], ["CX10", "CX11"])
     cp(T.PK[:, 3072:4096], T.RES[:, 0:3344].indirect(T.EO[:, 192:256]), ["RES", "RESZ", "EO"], ["PKx"])
     last_constants()
     for j in range(4):
@@ -323,16 +324,20 @@ def rank_program(g, core, T, topo):
         cp(T.P0[:], T.PK[:, 0:4096:16], ["PK", "PKx"], ["P0"])
         v(lambda: V.memset(T.PK[:, 0:4096:16], 255.0), [], ["PK"])
         mm(T.B1[:, 0:256], T.KC[0:1, :], T.ONES[0:1, :], True, False, ["KC", "ONES"], ["B1.ks"])
-        for j in range(4):
-            s = slice(1024 * j, 1024 * j + 1024)
-            scan(T.CM[:, s], T[cx][:, s], T.PK[:, s], A.min, A.max, [cx, "PK"], ["CM%d" % j])
-            tt(T.CM[:, 1024 * j:1024 * j + 1024:16], T.P0[:, 64 * j:64 * j + 64], T.B0[:, 64 * j:64 * j + 64], A.max, ["P0", "B0.cap"], ["CM%d" % j])
-            for k in range(16):
-                mm(T.B1[:, 64 * j:64 * j + 64], T.D16[:, 15 - k:143 - k], T.CM[:, 1024 * j + k:1024 * j + 1024:16], False, j == 3 and k == 15,
+        mm(T.B1[:, 0:256], T.D16[:, 15:143], T.CAP[:, c:2048:8], False, False, ["D16", "CAP"], ["B1.ks"])
+        mm(T.B3[:, 256:512], T.ID[:], T.P0[:], True, False, ["ID", "P0"], ["B3.z"])
+        mm(T.B3[:, 256:512], T.NID[:], T.CAP[:, c:2048:8], False, True, ["NID", "CAP"], ["B3.z"])
+        act(T.R0[:], T.B3[:, 256:512], ["B3.z"], ["R0"], F.Relu)
+        for j in range(2):
+            s = slice(2048 * j, 2048 * j + 2048)
+            scan(T.CM[:, s], T[cx][:, s], T.PK[:, s], A.min, A.max, ["%s%d" % (cx, j), "PK"], ["CM%d" % j])
+            for k in range(1, 16):
+                mm(T.B1[:, 128 * j:128 * j + 128], T.D16[:, 15 - k:143 - k], T.CM[:, 2048 * j + k:2048 * j + 2048:16], False, False,
                    ["D16", "CM%d" % j], ["B1.ks"])
+        mm(T.B1[:, 0:256], T.D16[:, 15:143], T.R0[:], False, True, ["D16", "R0"], ["B1.ks"])
         cp(T.PK[:, 0:4096:16], T.P0[:], ["P0"], ["PK"])
         if 1 < t < NT:
-            cap_wide(t + 1)
+            cap_wide(t + 1, 1)
         if t > 1:
             set_words()
         else:
@@ -355,19 +360,19 @@ def rank_program(g, core, T, topo):
         ts(T.XB[:], T.XI2[:], -1.0, 15.0, A.mult, A.add, ["XI2"], ["XB"])
         to_list(0, "XB", [T.XB], "B4.kl", False)
         tt(T.M1[:], T.FB[:, 15:4096:16], T.B2[:, 0:256], A.min, ["FB", "B2.c1"], ["M1"])
-        ts(T.B0[:, 256:512], T.M1[:], 0.0, None, A.max, None, ["M1"], ["B0.m1"])
+        act(T.B0[:, 256:512], T.M1[:], ["M1"], ["B0.m1"], F.Relu)
         if t < NT:
             offsets_b(t + 1)
         new_words()
-        act(T.R1[:], T.B2[:, 0:256], ["B2.c1"], ["R1"], F.Relu, scale=4096.0)
-        if t < NT:
-            parity()
+        act(T.R0[:], T.B2[:, 0:256], ["B2.c1"], ["R0"], F.Relu, scale=4096.0)
         cp(T.KL[:], T.B4[:, 0:16], ["B4.kl"], ["KL"])
         v(lambda: V.tensor_copy(T.PK[:, 0:4096].indirect(T.KL[:, 0:16]), T.ZER[:]), ["KL", "ZER"], ["PK"])
         scan(T.FB[:], T.SEG[:], T.PK[:, 0:4096], A.mult, A.max, ["SEG", "PK"], ["FB"])
         tt(T.CMP2[:], T.FB[:, 15:4096:16], T.B0[:, 0:256], A.is_gt, ["FB", "B0.cap"], ["CMP2"])
         mm(T.B3[:, 0:256], T.LIMT[:], T.ONES[:], True, False, ["LIMT", "ONES"], ["B3.c2"])
         mm(T.B3[:, 0:256], T.NBO[:], T.CMP2[:], False, True, ["NBO", "CMP2"], ["B3.c2"])
+        if t < NT:
+            parity()
         tt(T.M2[:], T.FB[:, 15:4096:16], T.B3[:, 0:256], A.min, ["FB", "B3.c2"], ["M2"])
         tt(snd, T.M2[:], T.B0[:, 256:512], A.max, ["M2", "B0.m1"], [sk])
         dst = cores[(rank + 1 + c % (n - 1)) % n]
@@ -395,7 +400,7 @@ def rank_program(g, core, T, topo):
             act(T.MX[:, 1024 * j:1024 * j + 1024], land.indirect(T.OFFC[:, 64 * j:64 * j + 64]), [lk, "OFFC"], ["MX%d" % j])
         mm(T.B3[:, 256:512], T.NID[:], T.N16B[:], True, False, ["NID", "N16B"], ["B3.z"])
         mm(T.B3[:, 256:512], T.N20[:], T.NEB[:], False, False, ["N20", "NEB"], ["B3.z"])
-        mm(T.B3[:, 256:512], T.NID[:], T.R1[:], False, True, ["NID", "R1"], ["B3.z"])
+        mm(T.B3[:, 256:512], T.NID[:], T.R0[:], False, True, ["NID", "R0"], ["B3.z"])
         cp(T.UI[:], T.B5[:, 0:256], ["B5.u"], ["UI"])
         ts(T.UU[:], T.UI[:], 4095, None, A.bitwise_and, None, ["UI"], ["UU"])
         ts(T.B5[:, 256:512], T.UU[:], T.KAF[:, 0:1], None, A.mult, None, ["UU", "KAF"], ["B5.fu"])
@@ -408,8 +413,9 @@ def rank_program(g, core, T, topo):
         if t < NT:
             act(T.RES[:, 2048 + L0:2048 + L0 + Q], land, [lk], ["RES"])
             bulk()
+            cap_wide(t + 1, 0)
         if t == 1:
-            cap_wide(2)
+            cap_wide(2, 1)
         mm(T.B6[:, 0:256], T.NEG[:], T.ONES[:], True, False, ["NEG", "ONES"], ["B6.x"])
         mm(T.B6[:, 0:256], T.KC2[0:1, :], T.ONES[0:1, :], False, False, ["KC2", "ONES"], ["B6.x"])
         for j in range(4):
@@ -433,12 +439,11 @@ def rank_program(g, core, T, topo):
         scan(T.KRV[:, ::-1], T.RM[:, ::-1], T.VS[:, ::-1], A.mult, A.max, ["RM", "VS"], ["KRV"])
         v(lambda: V.transpose(T.KB[:], T.KRV[:]), ["KRV"], ["KB"])
         cp(T.VB[:], T.KB[:], ["KB"], ["VB"])
-        for q in range(2):
-            for i in range(8 * q, 8 * q + 8):
-                ts(T.EQ[:, i, 0:256 - 16 * i], T.VB[:, 16 * i:256], T.B4[:, 32 + i:33 + i], None, A.is_equal, None, ["VB", "B4.lv"], ["EQ%d" % q])
-            tt(T.EQ[:, 8 * q:8 * q + 8, 0:16], T.EQ[:, 8 * q:8 * q + 8, 0:16], T.TRI[:, 8 * q:8 * q + 8, :], A.mult, ["EQ%d" % q, "TRI"], ["EQ%d" % q])
-            for i in range(8 * q, 8 * q + 8):
-                mm(T.B7[:, 16 * i:256], T.BO4[:], T.EQ[:, i, 0:256 - 16 * i], False, i == 15, ["BO4", "EQ%d" % q], ["B7.x"])
+        for i in range(16):
+                ts(T.EQ[:, i, 0:256 - 16 * i], T.VB[:, 16 * i:256], T.B4[:, 32 + i:33 + i], None, A.is_equal, None, ["VB", "B4.lv"], ["EQ%d" % i])
+                mm(T.B7[:, 16 * i:16 * i + 16], T.BT4[:], T.EQ[:, i, 0:16], False, i == 15, ["BT4", "EQ%d" % i], ["B7.x"])
+                if i < 15:
+                    mm(T.B7[:, 16 * i + 16:256], T.BO4[:], T.EQ[:, i, 16:256 - 16 * i], False, False, ["BO4", "EQ%d" % i], ["B7.x"])
         lv = T.B4[:, 32:48]
         if t < NT:
             ts(T.LW[:], T.B4[:, 48:64], float(t), 8192.0, A.not_equal, A.mult, ["B4.lv"], ["LW"])
@@ -460,5 +465,5 @@ def rank_program(g, core, T, topo):
     g.wait_ge(T.sem.loc, sum(len(topo.engines(core, cores[(rank + 1 + c % (n - 1)) % n])) for c in range(NT)))
     for s, k in own.items():
         g.wait_ge(T.sem[k], count[s])
-    for s in ("dyr", "dyb", "dtri", "dbr", "dres", "dcap", "dwt", "dka"):
+    for s in ("dyr", "dyb", "dbr", "dres", "dcap", "dwt", "dka"):
         g.wait_ge(T.sem[s], 16)

from concourse.mybir import AluOpType as A, ActivationFunctionType as F

NT = 6
Q = 256
ZC = 3328
TR = 4128
MAGIC = 12582912.0
SCRATCH = {
    "RES": ("sbuf", [128, 3344], "bfloat16"),
    "WD": ("sbuf", [128, 2304], "float32"),
    "BRI": ("sbuf", [128, 2048], "int32"),
    "PK": ("sbuf", [128, 4384], "bfloat16"),
    "EQ": ("sbuf", [128, 16, 256], "bfloat16"),
    "SND": ("sbuf", [128, NT * Q], "bfloat16"),
    "LAND": ("sbuf", [128, NT * Q], "bfloat16"),
    "D16": ("sbuf", [128, 144], "bfloat16"),
    "D32": ("sbuf", [128, 144], "bfloat16"),
    "SW0": ("sbuf", [128, 160], "bfloat16"),
    "SW1": ("sbuf", [128, 160], "bfloat16"),
    "IO256": ("sbuf", [128, 16], "bfloat16"),
    "XB": ("sbuf", [128, 16], "bfloat16"),
    "HB": ("sbuf", [128, 32], "bfloat16"),
    "HL": ("sbuf", [128, 32], "int32"),
    "XK": ("sbuf", [128, 8], "float32"),
}
for _n in ("FB", "CM", "CX0", "CX1", "MX", "SC", "SEG", "SP"):
    SCRATCH[_n] = ("sbuf", [128, 4096], "bfloat16")
for _n in ("CAP", "SL"):
    SCRATCH[_n] = ("sbuf", [128, 2048], "bfloat16")
for _n in ("CC", "P0", "ZER", "ONES", "IOBF", "OFFD", "CMP1", "CMP2", "M1", "M2", "SGN", "DELB", "DELI", "N12", "N16", "N16B", "BD1", "BD2", "NEB", "R0"):
    SCRATCH[_n] = ("sbuf", [128, 256], "bfloat16")
for _n in ("IOT", "IO16", "NDEL", "NEW", "MB", "RM", "OFS", "KT", "KSC", "KRV", "KB", "KEY", "VS", "CNS", "WOLD", "FA", "FM"):
    SCRATCH[_n] = ("sbuf", [128, 256], "float32")
for _n in ("BO", "NBO", "BO4", "BT4", "WTL", "ID", "NID", "N20", "IDT", "C37", "KC", "KC2", "KR16", "NEG", "FOUR", "LIMT"):
    SCRATCH[_n] = ("sbuf", [128, 128], "bfloat16")
for _n in ("IOB", "PAR"):
    SCRATCH[_n] = ("sbuf", [128, 128], "float32")
for _n in ("UI", "UU", "SQ", "PI2"):
    SCRATCH[_n] = ("sbuf", [128, 256], "int32")
for _n in ("EO", "P16", "VB", "OFFC"):
    SCRATCH[_n] = ("sbuf", [128, 256], "uint16")
for _n in ("WTI", "KAI", "PI", "KI", "HI"):
    SCRATCH[_n] = ("sbuf", [128, 1], "int32")
for _n in ("WTF", "KAF", "PF", "KF", "G16", "G15", "P16F", "H0", "H1", "SACC", "PA", "PB", "PC", "ODD"):
    SCRATCH[_n] = ("sbuf", [128, 1], "float32")
for _n in ("IL", "TP", "TW", "LX", "LW", "LB", "LC"):
    SCRATCH[_n] = ("sbuf", [128, 16], "float32")
for _n in ("XI", "XI2"):
    SCRATCH[_n] = ("sbuf", [128, 16], "int32")
for _n in ("KL", "PL", "PW"):
    SCRATCH[_n] = ("sbuf", [128, 16], "uint16")
for _n in range(8):
    SCRATCH["B%d" % _n] = ("psum", [128, 512], "float32")
SEMAPHORES = ["cv", "ct", "ca", "cp", "dbr", "dres", "dcap", "dwt", "dka", "dyr", "dyb", "loc"] + ["arr%d" % t for t in range(1, NT + 1)]


def rank_program(g, core, T, topo):
    rank = T.rank_of(core)
    if rank is None:
        return
    cores = T.cores
    n = len(cores)
    queues = {"v": g.vector, "t": g.tensor, "a": g.scalar, "p": g, "s": g.sync}
    own = {"v": "cv", "t": "ct", "a": "ca", "p": "cp"}
    count = {k: 0 for k in ("v", "t", "a", "p")}
    known = {k: {} for k in queues}
    lastw, readers, banks = {}, {}, {}

    def wait_for(eng, toks):
        best = {}
        for tok in toks:
            if tok[0] not in best or best[tok[0]][1] < tok[1]:
                best[tok[0]] = tok
        kn = known[eng]
        for s, val, snap in sorted(best.values(), key=lambda x: -len(x[2])):
            if kn.get(s, 0) >= val:
                continue
            queues[eng].wait_ge(T.sem[s], val)
            kn[s] = val
            for s2, v2 in snap.items():
                if kn.get(s2, 0) < v2:
                    kn[s2] = v2

    def banks_of(r, w):
        return set(x.split(".")[0] for x in list(r) + list(w) if "." in x)

    def deps(eng, r, w):
        toks = []
        for k in r:
            if k in lastw:
                toks.append(lastw[k])
        for k in w:
            if k in lastw:
                toks.append(lastw[k])
            toks += list(readers.get(k, {}).values())
        for k in banks_of(r, w):
            toks += [tok for e, tok in banks.get(k, {}).items() if e != eng]
        if eng == "t":
            toks = [x for x in toks if x[0] != "ct"]
        return toks

    def note(eng, tok, r, w):
        for k in r:
            readers.setdefault(k, {})[tok[0]] = tok
        for k in w:
            lastw[k] = tok
            readers[k] = {}
        for k in banks_of(r, w):
            banks.setdefault(k, {})[eng] = tok

    def op(eng, f, r, w):
        wait_for(eng, deps(eng, r, w))
        count[eng] += 1
        tok = (own[eng], count[eng], dict(known[eng]))
        f().then_inc(T.sem[own[eng]], 1)
        note(eng, tok, r, w)

    def dma(eng, out, in_, sem, r, w):
        wait_for(eng, deps(eng, r, w))
        queues[eng].dma_start(out, in_).then_inc(T.sem[sem], 16)
        note(eng, (sem, 16, dict(known[eng])), r, w)

    V, PE, AC = g.vector, g.tensor, g.scalar

    def v(f, r, w):
        op("v", f, r, w)

    def mm(out, lhs, rhs, st, sp, r, w):
        op("t", lambda: PE.matmul(out, lhs, rhs, st, sp), r, w)

    def act(out, in_, r, w, func=F.Copy, bias=0.0, scale=1.0):
        op("a", lambda: AC.activation(out, in_, func, bias=bias, scale=scale), r, w)

    def fill(ap, c, k):
        v(lambda: V.memset(ap, c), [], [k])

    def pfill(ap, c, k, cols):
        op("p", lambda: g.iota(ap, [[0, cols]], c, 0, allow_small_or_imprecise_dtypes=True), [], [k])

    def ts(out, in0, s1, s2, o0, o1, r, w):
        if o1 is None:
            v(lambda: V.tensor_scalar(out, in0, s1, None, o0), r, w)
        else:
            v(lambda: V.tensor_scalar(out, in0, s1, s2, o0, o1), r, w)

    def tt(out, a, b, o, r, w):
        v(lambda: V.tensor_tensor(out, a, b, o), r, w)

    def cp(out, a, r, w):
        v(lambda: V.tensor_copy(out, a), r, w)

    def scan(out, d0, d1, o0, o1, r, w):
        v(lambda: V.tensor_tensor_scan(out, d0, d1, 0.0, o0, o1), r, w)

    dma("s", T.BRI[:], T.br[:], "dbr", [], ["BRI"])
    dma("a", T.RES[:, 0:ZC], T.res[:], "dres", [], ["RES"])
    dma("s", T.CAP[:], T.cap[:], "dcap", [], ["CAP"])
    dma("s", T.WTI[:], T.wt[:], "dwt", [], ["WTI"])
    dma("s", T.KAI[:], T.ka[:], "dka", [], ["KAI"])
    op("p", lambda: g.iota(T.PI[:], [[0, 1]], 0, 1), [], ["PI"])
    op("p", lambda: g.iota(T.IOT[:], [[1, 256]], 0, 0, allow_small_or_imprecise_dtypes=True), [], ["IOT"])
    op("p", lambda: g.iota(T.IO16[:], [[0, 16], [1, 16]], 0, 0, allow_small_or_imprecise_dtypes=True), [], ["IO16"])
    op("p", lambda: g.iota(T.IOB[:], [[16, 8], [0, 16]], 0, 0, allow_small_or_imprecise_dtypes=True), [], ["IOB"])
    pfill(T.SP[:], 0, "SP", 4096)
    pfill(T.ONES[:], 1, "ONES", 256)
    pfill(T.LIMT[:], 18, "LIMT", 128)
    pfill(T.ZER[:], 0, "ZER", 256)
    pfill(T.VS[:], 0, "VS", 256)
    pfill(T.PAR[:], 1, "PAR", 128)
    pfill(T.FOUR[:], 4, "FOUR", 128)
    pfill(T.C37[:], 37, "C37", 128)
    pfill(T.NEG[:], -131072, "NEG", 128)
    fill(T.RES[:, ZC:ZC + 16], 0.0, "RESZ")
    fill(T.SEG[:], 1.0, "SEG")
    fill(T.SEG[:, 0:4096:16], 0.0, "SEG")
    fill(T.MB[:], 1e9, "MB")
    fill(T.MB[:, 0:256:16], -1e9, "MB")
    fill(T.RM[:], 1.0, "RM")
    fill(T.RM[:, 15:256:16], 0.0, "RM")
    act(T.KC[:], T.IO16[:, 0:128], ["IO16"], ["KC"], bias=15.0, scale=-1.0)
    act(T.KC2[:], T.IO16[:, 0:128], ["IO16"], ["KC2"], bias=30720.0, scale=-2048.0)
    act(T.KR16[:], T.IO16[:, 0:128], ["IO16"], ["KR16"], scale=16.0)
    act(T.IO256[:], T.IOT[:, 0:16], ["IOT"], ["IO256"], scale=256.0)
    act(T.IOBF[:], T.IOT[:], ["IOT"], ["IOBF"])
    ts(T.KI[:], T.PI[:], 15, None, A.bitwise_and, None, ["PI"], ["KI"])
    ts(T.HI[:], T.PI[:], 16, None, A.bitwise_and, None, ["PI"], ["HI"])
    cp(T.PF[:], T.PI[:], ["PI"], ["PF"])
    cp(T.KF[:], T.KI[:], ["KI"], ["KF"])
    tt(T.G16[:], T.PF[:], T.KF[:], A.subtract, ["PF", "KF"], ["G16"])
    ts(T.G15[:], T.G16[:], 15.0, None, A.add, None, ["G16"], ["G15"])
    ts(T.P16F[:], T.PF[:], 16.0, None, A.add, None, ["PF"], ["P16F"])
    ts(T.H1[:], T.HI[:], 0.0625, None, A.mult, None, ["HI"], ["H1"])
    ts(T.H0[:], T.HI[:], -0.0625, 1.0, A.mult, A.add, ["HI"], ["H0"])
    ts(T.D16[:], T.IOT[:, 0:144], T.G15[:, 0:1], 16.0, A.is_equal, A.mult, ["IOT", "G15"], ["D16"])
    ts(T.NBO[:], T.IOB[:], T.G16[:, 0:1], -512.0, A.is_equal, A.mult, ["IOB", "G16"], ["NBO"])

    def one_hot(out, off, pos, value, r, w):
        if value is None:
            ts(out, off, pos, None, A.is_equal, None, r, w)
        else:
            ts(out, off, pos, value, A.is_equal, A.mult, r, w)

    def more_constants():
        one_hot(T.ID[:], T.IOT[:, 0:128], T.PF[:, 0:1], None, ["IOT", "PF"], ["ID"])
        one_hot(T.SW0[:], T.IOT[:, 0:160], T.P16F[:, 0:1], T.H0[:, 0:1], ["IOT", "P16F", "H0"], ["SW0"])
        one_hot(T.SW1[:], T.IOT[:, 0:160], T.P16F[:, 0:1], T.H1[:, 0:1], ["IOT", "P16F", "H1"], ["SW1"])
        one_hot(T.DELB[:], T.IO16[:], T.KF[:, 0:1], None, ["IO16", "KF"], ["DELB"])
        ts(T.BT4[:], T.IO16[:, 0:128], T.KF[:, 0:1], 8192.0, A.is_gt, A.mult, ["IO16", "KF"], ["BT4"])
        act(T.BO[:], T.NBO[:], ["NBO"], ["BO"], scale=-0.001953125)
        act(T.NID[:], T.ID[:], ["ID"], ["NID"], scale=-1.0)
        act(T.N20[:], T.ID[:], ["ID"], ["N20"], scale=-1048576.0)
        act(T.BO4[:], T.NBO[:], ["NBO"], ["BO4"], scale=-16.0)
        act(T.D32[:], T.D16[:], ["D16"], ["D32"], scale=2048.0)
        act(T.NDEL[:], T.DELB[:], ["DELB"], ["NDEL"], bias=1.0, scale=-1.0)
        act(T.OFFD[:], T.DELB[:], ["DELB"], ["OFFD"], bias=-2097152.0, scale=2097152.0)
        op("a", lambda: AC.activation(T.IL[:], T.IOT[:, 0:16], F.Identity, bias=T.KF[:, 0:1], scale=16.0), ["IOT", "KF"], ["IL"])
        act(T.TP[:], T.IL[:], ["IL"], ["TP"], bias=float(TR))
        act(T.TW[:], T.IL[:], ["IL"], ["TW"], bias=2048.0)
        op("a", lambda: AC.activation(T.XK[:], T.IOT[:, 0:8], F.Identity, bias=T.KF[:, 0:1], scale=-2.0), ["IOT", "KF"], ["XK"])

    def last_constants():
        tt(T.BT4[:], T.BT4[:], T.BO[:], A.mult, ["BT4", "BO"], ["BT4"])
        tt(T.DELI[:], T.IOT[:], T.DELB[:], A.mult, ["IOT", "DELB"], ["DELI"])
        cp(T.OFFC[:], T.IOT[:], ["IOT"], ["OFFC"])
        cp(T.WTF[:], T.WTI[:], ["WTI"], ["WTF"])
        cp(T.KAF[:], T.KAI[:], ["KAI"], ["KAF"])
        ts(T.WTL[:], T.BO[:], T.WTF[:, 0:1], None, A.mult, None, ["BO", "WTF"], ["WTL"])

    def floors(src, size, out, ok, sign):
        act(T.FA[:], src, ["WD"], ["FA"], bias=-0.5 + 0.5 / size, scale=1.0 / size)
        act(T.FM[:], T.FA[:], ["FA"], ["FM"], bias=MAGIC)
        act(out, T.FM[:], ["FM"], [ok], bias=-sign * size * MAGIC, scale=sign * size)

    def first_offsets():
        src = T.BRI[:, 0:2048:8]
        ts(T.OFS[:], src, 0.0, 4096.0, A.is_lt, A.mult, ["BRI"], ["OFS"])
        ts(T.UU[:], src, 65535, None, A.bitwise_and, None, ["BRI"], ["UU"])
        ts(T.UI[:], src, 4095, None, A.bitwise_and, None, ["BRI"], ["UI"])
        ts(T.KT[:], T.UU[:], 4096.0, 4096.0, A.is_lt, A.mult, ["UU"], ["KT"])
        tt(T.OFS[:], T.OFS[:], T.KT[:], A.max, ["OFS", "KT"], ["OFS"])
        tt(T.OFS[:], T.OFS[:], T.UI[:], A.max, ["OFS", "UI"], ["OFS"])
        ts(T.EO[:], T.OFS[:], float(ZC), None, A.min, None, ["OFS"], ["EO"])

    def offsets_a(t):
        w = T.WD[:, t - 1:2048:8]
        floors(w, 4096.0, T.N12[:], "N12", 1.0)
        floors(w, 65536.0, T.N16[:], "N16", -1.0)
        act(T.BD2[:], T.N16[:], ["N16"], ["BD2"], F.Relu, bias=-65536.0 * (t - 1))

    def offsets_b(t):
        mm(T.B6[:, 256:512], T.ID[:], T.N12[:], True, False, ["ID", "N12"], ["B6.t"])
        mm(T.B6[:, 256:512], T.ID[:], T.N16[:], False, True, ["ID", "N16"], ["B6.t"])
        act(T.BD1[:], T.B6[:, 256:512], ["B6.t"], ["BD1"], F.Relu, bias=4096.0 * t, scale=-1.0)
        mm(T.B2[:, 256:512], T.NID[:], T.N12[:], True, False, ["NID", "N12"], ["B2.off"])
        mm(T.B2[:, 256:512], T.ID[:], T.BD1[:], False, False, ["ID", "BD1"], ["B2.off"])
        mm(T.B2[:, 256:512], T.ID[:], T.BD2[:], False, True, ["ID", "BD2"], ["B2.off"])

    def offsets_c(t):
        tt(T.OFS[:], T.WD[:, t - 1:2048:8], T.B2[:, 256:512], A.add, ["WD", "B2.off"], ["OFS"])
        ts(T.EO[:], T.OFS[:], float(ZC), None, A.min, None, ["OFS"], ["EO"])

    def bulk():
        act(T.PK[:, 0:4096], T.RES[:, 0:3344].indirect(T.EO[:, 0:256]), ["RES", "RESZ", "EO"], ["PK"])

    def cap_room(t):
        act(T.B0[:, 0:256], T.CAP[:, t - 1:2048:8], ["CAP"], ["B0.cap"])

    def cap_wide(t, half):
        cx = "CX%d" % (t & 1)
        if half or t == 2:
            act(T.CC[:], T.CAP[:, t - 1:2048:8], ["CAP"], ["CC"])
        act(T[cx][:, 2048 * half:2048 * half + 2048], T.CC[:].indirect(T.OFFC[:, 128 * half:128 * half + 128]), ["CC", "OFFC"], ["%s%d" % (cx, half)])

    def to_list(col, key, parts, wkey, first):
        for ip in (0, 1):
            for h in (0, 1):
                sw, o = (T.SW0, (16, 0)[h]) if ip == 0 else (T.SW1, (32, 16)[h])
                for j, p in enumerate(parts):
                    mm(T.B4[:, col + ip:col + 16:2], sw[:, o:o + 128], p[:, h:16:2], first and h == 0 and j == 0,
                       (first or ip == 1) and h == 1 and j == len(parts) - 1, ["SW0", "SW1", key], [wkey])

    def set_words():
        tt(T.WOLD[:], T.WD[:, 0:2304].indirect(T.PW[:, 0:16]), T.NDEL[:], A.mult, ["WD", "PW", "NDEL"], ["WOLD"])
        tt(T.WD[:, 0:2304].indirect(T.PW[:, 0:16]), T.WOLD[:], T.NEW[:], A.add, ["WOLD", "NEW", "PW"], ["WD"])

    def suspended(t):
        tt(T.WD[:, t - 1:2048:8], T.WD[:, t - 1:2048:8], T.B3[:, 256:512], A.subtract, ["WD", "B3.z"], ["WD"])

    def parity():
        op("a", lambda: AC.activation(T.SGN[:], T.B2[:, 0:256], F.Sign, accum_out=T.SACC[:]), ["B2.c1"], ["SGN", "SACC"])
        mm(T.B5[:, 0:1], T.PAR[:], T.SACC[:], True, True, ["PAR", "SACC"], ["B5.par"])
        act(T.PA[:], T.B5[:, 0:1], ["B5.par"], ["PA"], scale=-0.03125)
        act(T.PB[:], T.PA[:], ["PA"], ["PB"], bias=-0.25, scale=0.5)
        act(T.PC[:], T.PB[:], ["PB"], ["PC"], bias=MAGIC)
        act(T.PB[:], T.PC[:], ["PC"], ["PB"], bias=2.0 * MAGIC, scale=-2.0)
        op("a", lambda: AC.activation(T.ODD[:], T.PB[:], F.Identity, bias=T.PA[:, 0:1]), ["PA", "PB"], ["ODD"])

    def new_words():
        mm(T.B7[:, 256:512], T.ID[:], T.DELI[:], True, False, ["ID", "DELI"], ["B7.n"])
        mm(T.B7[:, 256:512], T.IDT[:], T.DELB[:], False, True, ["IDT", "DELB"], ["B7.n"])
        act(T.NEW[:], T.B7[:, 256:512], ["B7.n"], ["NEW"])

    more_constants()
    first_offsets()
    act(T.PK[:, 0:3072], T.RES[:, 0:3344].indirect(T.EO[:, 0:192]), ["RES", "RESZ", "EO"], ["PK"])
    cap_room(1)
    cp(T.SP[:, 0:4096:16], T.CAP[:, 0:2048:8], ["CAP"], ["SP"])
    scan(T.CX1[:], T.SEG[:], T.SP[:], A.mult, A.max, ["SEG", "SP"], ["CX10", "CX11"])
    cp(T.PK[:, 3072:4096], T.RES[:, 0:3344].indirect(T.EO[:, 192:256]), ["RES", "RESZ", "EO"], ["PKx"])
    last_constants()
    for j in range(4):
        b, k = (T.B5, "B5.x") if j % 2 else (T.B7, "B7.x")
        s = slice(512 * j, 512 * j + 512)
        mm(b[:], T.ID[:], T.CAP[:, s], True, False, ["ID", "CAP"], [k])
        mm(b[:], T.NID[:], T.RES[:, s], False, True, ["NID", "RES"], [k])
        act(T.SL[:, s], b[:], [k], ["SL"], F.Relu)

    for t in range(1, NT + 1):
        c = t - 1
        cx = "CX%d" % (t & 1)
        L0 = c * Q
        land, lk = T.LAND[:, L0:L0 + Q], "LAND%d" % t
        snd, sk = T.SND[:, L0:L0 + Q], "SND%d" % t
        cp(T.P0[:], T.PK[:, 0:4096:16], ["PK", "PKx"], ["P0"])
        v(lambda: V.memset(T.PK[:, 0:4096:16], 255.0), [], ["PK"])
        mm(T.B1[:, 0:256], T.KC[0:1, :], T.ONES[0:1, :], True, False, ["KC", "ONES"], ["B1.ks"])
        mm(T.B1[:, 0:256], T.D16[:, 15:143], T.CAP[:, c:2048:8], False, False, ["D16", "CAP"], ["B1.ks"])
        mm(T.B3[:, 256:512], T.ID[:], T.P0[:], True, False, ["ID", "P0"], ["B3.z"])
        mm(T.B3[:, 256:512], T.NID[:], T.CAP[:, c:2048:8], False, True, ["NID", "CAP"], ["B3.z"])
        act(T.R0[:], T.B3[:, 256:512], ["B3.z"], ["R0"], F.Relu)
        for j in range(2):
            s = slice(2048 * j, 2048 * j + 2048)
            scan(T.CM[:, s], T[cx][:, s], T.PK[:, s], A.min, A.max, ["%s%d" % (cx, j), "PK"], ["CM%d" % j])
            for k in range(1, 16):
                mm(T.B1[:, 128 * j:128 * j + 128], T.D16[:, 15 - k:143 - k], T.CM[:, 2048 * j + k:2048 * j + 2048:16], False, False,
                   ["D16", "CM%d" % j], ["B1.ks"])
        mm(T.B1[:, 0:256], T.D16[:, 15:143], T.R0[:], False, True, ["D16", "R0"], ["B1.ks"])
        cp(T.PK[:, 0:4096:16], T.P0[:], ["P0"], ["PK"])
        if 1 < t < NT:
            cap_wide(t + 1, 1)
        if t > 1:
            set_words()
        else:
            cp(T.WD[:, 0:2048], T.BRI[:], ["BRI"], ["WD"])
            fill(T.WD[:, 2048:2304], 0.0, "WD")
        if t < NT:
            offsets_a(t + 1)
        floors(T.WD[:, c:2048:8], 65536.0, T.N16B[:], "N16B", -1.0)
        act(T.IDT[:], T.ID[:], ["ID"], ["IDT"], scale=2048.0 + 256.0 * c + 4096.0 * (t + 2))
        scan(T.FB[:], T.SEG[:], T.PK[:, 0:4096], A.mult, A.max, ["SEG", "PK"], ["FB"])
        tt(T.CMP1[:], T.FB[:, 15:4096:16], T.B0[:, 0:256], A.is_gt, ["FB", "B0.cap"], ["CMP1"])
        mm(T.B2[:, 0:256], T.LIMT[:], T.ONES[:], True, False, ["LIMT", "ONES"], ["B2.c1"])
        mm(T.B2[:, 0:256], T.NBO[:], T.CMP1[:], False, True, ["NBO", "CMP1"], ["B2.c1"])
        mm(T.B4[:, 0:16], T.KR16[0:1, :], T.ONES[0:1, 0:16], True, False, ["KR16", "ONES"], ["B4.kl"])
        mm(T.B4[:, 0:16], T.ONES[0:1, 0:128], T.IO256[0:1, :], False, False, ["IO256", "ONES"], ["B4.kl"])
        v(lambda: V.transpose(T.KT[:], T.B1[:, 0:256]), ["B1.ks"], ["KT"])
        scan(T.KSC[:], T.MB[:], T.KT[:], A.min, A.max, ["MB", "KT"], ["KSC"])
        cp(T.XI[:], T.KSC[:, 15:256:16], ["KSC"], ["XI"])
        ts(T.XI2[:], T.XI[:], 15, None, A.bitwise_and, None, ["XI"], ["XI2"])
        ts(T.XB[:], T.XI2[:], -1.0, 15.0, A.mult, A.add, ["XI2"], ["XB"])
        to_list(0, "XB", [T.XB], "B4.kl", False)
        tt(T.M1[:], T.FB[:, 15:4096:16], T.B2[:, 0:256], A.min, ["FB", "B2.c1"], ["M1"])
        act(T.B0[:, 256:512], T.M1[:], ["M1"], ["B0.m1"], F.Relu)
        if t < NT:
            offsets_b(t + 1)
        new_words()
        act(T.R0[:], T.B2[:, 0:256], ["B2.c1"], ["R0"], F.Relu, scale=4096.0)
        cp(T.KL[:], T.B4[:, 0:16], ["B4.kl"], ["KL"])
        v(lambda: V.tensor_copy(T.PK[:, 0:4096].indirect(T.KL[:, 0:16]), T.ZER[:]), ["KL", "ZER"], ["PK"])
        scan(T.FB[:], T.SEG[:], T.PK[:, 0:4096], A.mult, A.max, ["SEG", "PK"], ["FB"])
        tt(T.CMP2[:], T.FB[:, 15:4096:16], T.B0[:, 0:256], A.is_gt, ["FB", "B0.cap"], ["CMP2"])
        mm(T.B3[:, 0:256], T.LIMT[:], T.ONES[:], True, False, ["LIMT", "ONES"], ["B3.c2"])
        mm(T.B3[:, 0:256], T.NBO[:], T.CMP2[:], False, True, ["NBO", "CMP2"], ["B3.c2"])
        if t < NT:
            parity()
        tt(T.M2[:], T.FB[:, 15:4096:16], T.B3[:, 0:256], A.min, ["FB", "B3.c2"], ["M2"])
        tt(snd, T.M2[:], T.B0[:, 256:512], A.max, ["M2", "B0.m1"], [sk])
        dst = cores[(rank + 1 + c % (n - 1)) % n]
        rid, pid, _s = topo.addr(dst)
        wait_for("p", deps("p", [sk], []))
        g.remote_dma(land, snd, T.sem["arr%d" % t], T.sem.loc, pid, rid, topo.mask(core, dst))
        lastw[lk] = ("arr%d" % t, len(topo.engines(core, dst)), {})
        mm(T.B5[:, 256:512], T.ID[:], T.CAP[:, c:2048:8], True, False, ["ID", "CAP"], ["B5.sl"])
        mm(T.B5[:, 256:512], T.NID[:], snd, False, True, ["NID", sk], ["B5.sl"])
        act(T.SL[:, c:2048:8], T.B5[:, 256:512], ["B5.sl"], ["SL"], F.Relu)
        act(T.RES[:, c:2048:8], snd, [sk], ["RES"])
        if t == NT:
            dma("s", T.yr[:], T.RES[:, 0:2048], "dyr", ["RES"], ["yr"])
        if t < NT:
            cap_room(t + 1)
            op("a", lambda: AC.activation(T.LIMT[:], T.FOUR[:], F.Copy, bias=18.0, scale=T.ODD[:, 0:1]), ["FOUR", "ODD"], ["LIMT"])
        scan(T.KRV[:, ::-1], T.RM[:, ::-1], T.KSC[:, ::-1], A.mult, A.max, ["RM", "KSC"], ["KRV"])
        v(lambda: V.transpose(T.KB[:], T.KRV[:]), ["KRV"], ["KB"])
        tt(T.NEB[:], T.B1[:, 0:256], T.KB[:], A.not_equal, ["B1.ks", "KB"], ["NEB"])
        if t < NT:
            offsets_c(t + 1)
        mm(T.B5[:, 0:256], T.C37[0:1, :], T.IOBF[0:1, :], True, False, ["C37", "IOBF"], ["B5.u"])
        mm(T.B5[:, 0:256], T.WTL[:], land, False, True, ["WTL", lk], ["B5.u"])
        for j in range(4):
            act(T.MX[:, 1024 * j:1024 * j + 1024], land.indirect(T.OFFC[:, 64 * j:64 * j + 64]), [lk, "OFFC"], ["MX%d" % j])
        mm(T.B3[:, 256:512], T.NID[:], T.N16B[:], True, False, ["NID", "N16B"], ["B3.z"])
        mm(T.B3[:, 256:512], T.N20[:], T.NEB[:], False, False, ["N20", "NEB"], ["B3.z"])
        mm(T.B3[:, 256:512], T.NID[:], T.R0[:], False, True, ["NID", "R0"], ["B3.z"])
        cp(T.UI[:], T.B5[:, 0:256], ["B5.u"], ["UI"])
        ts(T.UU[:], T.UI[:], 4095, None, A.bitwise_and, None, ["UI"], ["UU"])
        ts(T.B5[:, 256:512], T.UU[:], T.KAF[:, 0:1], None, A.mult, None, ["UU", "KAF"], ["B5.fu"])
        tt(T.SQ[:], T.UU[:], T.UU[:], A.mult, ["UU"], ["SQ"])
        ts(T.SQ[:], T.SQ[:], 5, None, A.arith_shift_right, None, ["SQ"], ["SQ"])
        tt(T.PI2[:], T.SQ[:], T.B5[:, 256:512], A.add, ["SQ", "B5.fu"], ["PI2"])
        ts(T.PI2[:], T.PI2[:], 2047, None, A.bitwise_and, None, ["PI2"], ["PI2"])
        cp(T.P16[:], T.PI2[:], ["PI2"], ["P16"])
        act(T.B3[:, 256:512], T.B3[:, 256:512], ["B3.z"], ["B3.z"], F.Relu, bias=65536.0 * (t + 8))
        if t < NT:
            act(T.RES[:, 2048 + L0:2048 + L0 + Q], land, [lk], ["RES"])
            bulk()
            cap_wide(t + 1, 0)
        if t == 1:
            cap_wide(2, 1)
        mm(T.B6[:, 0:256], T.NEG[:], T.ONES[:], True, False, ["NEG", "ONES"], ["B6.x"])
        mm(T.B6[:, 0:256], T.KC2[0:1, :], T.ONES[0:1, :], False, False, ["KC2", "ONES"], ["B6.x"])
        for j in range(4):
            s = slice(1024 * j, 1024 * j + 1024)
            tt(T.SC[:, s], T.SL[:, 0:2048].indirect(T.P16[:, 64 * j:64 * j + 64]), T.MX[:, s], A.min, ["SL", "P16", "MX%d" % j], ["SC%d" % j])
            for k in range(16):
                mm(T.B6[:, 64 * j:64 * j + 64], T.D32[:, 15 - k:143 - k], T.SC[:, 1024 * j + k:1024 * j + 1024:16], False, j == 3 and k == 15,
                   ["D32", "SC%d" % j], ["B6.x"])
        mm(T.B7[:, 0:256], T.ID[:], T.OFFD[:], True, False, ["ID", "OFFD"], ["B7.x"])
        suspended(t)
        tt(T.KEY[:], T.B6[:, 0:256], T.PI2[:], A.add, ["B6.x", "PI2"], ["KEY"])
        v(lambda: V.transpose(T.KT[:], T.KEY[:]), ["KEY"], ["KT"])
        scan(T.KSC[:], T.MB[:], T.KT[:], A.min, A.max, ["MB", "KT"], ["KSC"])
        cp(T.XI[:], T.KSC[:, 15:256:16], ["KSC"], ["XI"])
        ts(T.HL[:, 0:16], T.XI[:], 2040, None, A.bitwise_and, None, ["XI"], ["HLa"])
        ts(T.HL[:, 16:32], T.XI[:], 7, None, A.bitwise_and, None, ["XI"], ["HLb"])
        cp(T.HB[:], T.HL[:], ["HLa", "HLb"], ["HB"])
        to_list(32, "HB", [T.HB, T.HB[:, 16:32]], "B4.lv", True)
        to_list(48, "HB", [T.HB[:, 16:32]], "B4.lv", True)
        tt(T.VS[:, 15:256:16], T.HL[:, 0:16], T.HL[:, 16:32], A.add, ["HLa", "HLb"], ["VS"])
        scan(T.KRV[:, ::-1], T.RM[:, ::-1], T.VS[:, ::-1], A.mult, A.max, ["RM", "VS"], ["KRV"])
        v(lambda: V.transpose(T.KB[:], T.KRV[:]), ["KRV"], ["KB"])
        cp(T.VB[:], T.KB[:], ["KB"], ["VB"])
        for i in range(16):
                ts(T.EQ[:, i, 0:256 - 16 * i], T.VB[:, 16 * i:256], T.B4[:, 32 + i:33 + i], None, A.is_equal, None, ["VB", "B4.lv"], ["EQ%d" % i])
                mm(T.B7[:, 16 * i:16 * i + 16], T.BT4[:], T.EQ[:, i, 0:16], False, i == 15, ["BT4", "EQ%d" % i], ["B7.x"])
                if i < 15:
                    mm(T.B7[:, 16 * i + 16:256], T.BO4[:], T.EQ[:, i, 16:256 - 16 * i], False, False, ["BO4", "EQ%d" % i], ["B7.x"])
        lv = T.B4[:, 32:48]
        if t < NT:
            ts(T.LW[:], T.B4[:, 48:64], float(t), 8192.0, A.not_equal, A.mult, ["B4.lv"], ["LW"])
            ts(T.LX[:], lv, 2.0, T.XK[:, t:t + 1], A.mult, A.add, ["B4.lv", "XK"], ["LX"])
            tt(T.LW[:], T.LW[:], T.TP[:], A.min, ["LW", "TP"], ["LW"])
            tt(T.LX[:], T.LW[:], T.LX[:], A.max, ["LW", "LX"], ["LX"])
        scan(T.CNS[:], T.MB[:], T.B7[:, 0:256], A.min, A.max, ["MB", "B7.x"], ["CNS"])
        if t < NT:
            tt(T.LB[:], T.CNS[:, 15:256:16], T.TP[:], A.min, ["CNS", "TP"], ["LB"])
            tt(T.LC[:], T.LB[:], T.LX[:], A.max, ["LB", "LX"], ["LC"])
            cp(T.PL[:], T.LC[:], ["LC"], ["PL"])
            v(lambda: V.tensor_copy(T.PK[:, 0:4384].indirect(T.PL[:, 0:16]), land), ["PL", lk], ["PK"])
        tt(T.LB[:], T.CNS[:, 15:256:16], T.TW[:], A.min, ["CNS", "TW"], ["LB"])
        tt(T.LC[:], T.LB[:], lv, A.max, ["LB", "B4.lv"], ["LC"])
        cp(T.PW[:], T.LC[:], ["LC"], ["PW"])

    set_words()
    dma("s", T.yb[:], T.WD[:, 0:2048], "dyb", ["WD"], ["yb"])
    g.wait_ge(T.sem.loc, sum(len(topo.engines(core, cores[(rank + 1 + c % (n - 1)) % n])) for c in range(NT)))
    for s, k in own.items():
        g.wait_ge(T.sem[k], count[s])
    for s in ("dyr", "dyb", "dbr", "dres", "dcap", "dwt", "dka"):
        g.wait_ge(T.sem[s], 16)
